import numpy as np
import ml_dtypes


def mxq(x, axis, fmt="e4m3"):
    dtype, down = {"e4m3": (ml_dtypes.float8_e4m3fn, 7), "e5m2": (ml_dtypes.float8_e5m2, 14)}[fmt]
    v = np.moveaxis(np.asarray(x, np.float32).astype(ml_dtypes.bfloat16).astype(np.float64), axis, -1)
    blocks = v.reshape(v.shape[:-1] + (-1, 32))
    amax = np.abs(blocks).max(-1, keepdims=True)
    byte = np.maximum(np.where(amax > 0, np.frexp(amax)[1] - 1 + 127, 0) - down, 1)
    scale = np.exp2(byte - 127.0)
    codes = (blocks / scale).astype(np.float32).astype(dtype).astype(np.float64)
    return np.moveaxis((codes * scale).reshape(v.shape), -1, axis)


WIDE = False


def mx_kscale(k):
    if not WIDE:
        return np.ones(k)
    levels = np.array([10, -10, 5, -5, 0])
    if k % 512:
        return np.exp2(np.random.permutation(np.resize(levels, k // 32))).repeat(32)
    a = np.empty((k // 512, 16))
    for p in range(k // 512):
        a[p, :8] = np.random.permutation(np.resize(levels, 8))
        for g in range(8):
            far = levels[np.abs(levels - a[p, g]) >= 10]
            a[p, g + 8] = far[np.random.randint(len(far))]
    return np.exp2(a.ravel()).repeat(32)


def f64(x):
    return np.asarray(x).astype(np.float64)


def striped(idx):
    return np.tile(idx.reshape(-1, 16).T, (8, 1)).astype(np.uint16)


def unstriped(offs):
    return offs[:16].T.reshape(-1).astype(np.int64)


E2M1 = np.array([0.0, 0.5, 1.0, 1.5, 2.0, 3.0, 4.0, 6.0, -0.0, -0.5, -1.0, -1.5, -2.0, -3.0, -4.0, -6.0])


def pack_weight(w, fmt):
    k, n = w.shape
    w = f64(np.asarray(w, np.float32).astype(ml_dtypes.bfloat16)).reshape(k // 32, 32, n)
    amax = np.abs(w).max(1)
    if fmt == "e4m3":
        byte = np.frexp(amax)[1] - 1 + 127 - 7
    else:
        mant, ex = np.frexp(amax / 6.0)
        byte = np.where(mant > 0.5, ex, ex - 1) + 127
    byte = np.clip(np.where(amax > 0, byte, 1), 1, 254)
    scaled = (w * np.exp2(127.0 - byte)[:, None, :]).reshape(k, n).astype(np.float32)
    by_word = np.ascontiguousarray(scaled.reshape(k // 512, 128, 4, n).transpose(0, 1, 3, 2))
    if fmt == "e4m3":
        words = by_word.astype(ml_dtypes.float8_e4m3fn).view(np.uint8)
    else:
        c = by_word.astype(ml_dtypes.float4_e2m1fn).view(np.uint8) & 0xF
        words = (c[..., 0::2] | (c[..., 1::2] << 4)).reshape(k // 512, 128, 2 * n)
    return np.ascontiguousarray(words), np.ascontiguousarray(byte.astype(np.uint8).reshape(k // 512, 16, n))


def unpack_weight(words, scales, fmt):
    g, _, n = scales.shape
    words = np.ascontiguousarray(words).reshape(g, 128, n, -1)
    if fmt == "e4m3":
        vals = words.view(ml_dtypes.float8_e4m3fn).astype(np.float64)
    else:
        nib = np.empty((g, 128, n, 4), np.uint8)
        nib[..., 0::2] = words & 0xF
        nib[..., 1::2] = words >> 4
        vals = E2M1[nib]
    vals = vals * np.repeat(np.exp2(scales.astype(np.float64) - 127.0), 8, axis=1)[..., None]
    return vals.transpose(0, 1, 3, 2).reshape(g * 512, n)


def gelu(v):
    return 0.5 * v * (1.0 + np.tanh(np.sqrt(2.0 / np.pi) * (v + 0.044715 * v**3)))


K, K2, T, T2, S, H, N = 1024, 512, 4096, 2048, 1024, 1024, 512

def setup_inputs():
    n = np.random.standard_normal
    s, s2, u = mx_kscale(K)[:, None], mx_kscale(K2)[:, None], mx_kscale(H)[:, None]
    tab_words, tab_scales = pack_weight(n((K, T)) * s, "e4m3")
    tab2_words, tab2_scales = pack_weight(n((K2, T2)) * s2, "e4m3")
    wr_words, wr_scales = pack_weight(n((K2, H)) / np.sqrt(K + K2) / s2, "e4m3")
    wm_words, wm_scales = pack_weight(n((H, N)) / np.sqrt(H) / u, "e2m1")
    return {
        "tab_words": tab_words, "tab_scales": tab_scales,
        "tab2_words": tab2_words, "tab2_scales": tab2_scales,
        "offs": striped(np.random.permutation(T)[:S]),
        "offs2": striped(np.random.permutation(T2)[:S]),
        "ws": (n((K, H)) / np.sqrt(K + K2) / s).astype(np.float32),
        "wr_words": wr_words, "wr_scales": wr_scales,
        "b": (0.3 * n(H)).astype(np.float32),
        "gain": (np.exp(0.3 * n(H)) * u[:, 0]).astype(np.float32),
        "wm_words": wm_words, "wm_scales": wm_scales,
        "bm": (0.3 * n(N)).astype(np.float32),
    }

def reference(tab_words, tab_scales, tab2_words, tab2_scales, offs, offs2, ws, wr_words, wr_scales, b, gain, wm_words, wm_scales, bm):
    v = unpack_weight(tab_words, tab_scales, "e4m3")[:, unstriped(offs)]
    v2 = unpack_weight(tab2_words, tab2_scales, "e4m3")[:, unstriped(offs2)]
    wsq = mxq(f64(ws), 0, "e4m3")
    wr = unpack_weight(wr_words, wr_scales, "e4m3")
    wm = unpack_weight(wm_words, wm_scales, "e2m1")
    a = wsq.T @ v + wr.T @ v2
    h = np.tanh(a + f64(b)[:, None]) * f64(gain)[:, None]
    y = wm.T @ mxq(h, 0, "e4m3")
    return y + f64(bm)[:, None]

@@ -1,0 +1,222 @@
+from contextlib import ExitStack
+
+import concourse.mybir as mybir
+
+K, K2, T, T2, S, H, N = 1024, 512, 4096, 2048, 1024, 1024, 512
+FLOPS = 2 * S * (K * H + K2 * H + H * N)
+
+F32 = mybir.dt.float32
+BF16 = mybir.dt.bfloat16
+I32 = mybir.dt.int32
+U32 = mybir.dt.uint32
+U16 = mybir.dt.uint16
+U8 = mybir.dt.uint8
+FP8X4 = mybir.dt.float8_e4m3fn_x4
+FP4X4 = mybir.dt.float4_e2m1fn_x4
+ACT = mybir.ActivationFunctionType
+ALU = mybir.AluOpType
+
+P = 128
+PACK = 4
+KP = P * PACK
+NJ = 512
+TAB2_ROW = 8
+WR_ROW = 12
+LAST_SCALAR_M = 40
+
+
+def tile_list_bipartite_edge_messages_kernel(
+    tc, tab_words, tab_scales, tab2_words, tab2_scales, offs, offs2, ws, wr_words, wr_scales,
+    b, gain, wm_words, wm_scales, bm, out,
+):
+    nc = tc.nc
+    with ExitStack() as ctx:
+        keep = ctx.enter_context(tc.tile_pool(name="keep", bufs=1))
+        ring = ctx.enter_context(tc.tile_pool(name="ring", bufs=3))
+        psum = ctx.enter_context(tc.psum_pool(name="psum", bufs=1))
+
+        def held(name, shape, dtype):
+            return keep.tile(shape, dtype, name=name, align_bytes=64)
+
+        idx = keep.tile([P, S // 16], U16, name="idx")
+        idx2 = keep.tile([P, S // 16], U16, name="idx2")
+        tab_w = [held("tab_w%d" % a, [P, T], I32) for a in range(2)]
+        tab_s = held("tab_s", [P, T // 4], I32)
+        tab2_w = held("tab2_w", [P, T2], I32)
+        tab2_s = held("tab2_s", [P, T2 // 4], I32)
+        wr_w_in = held("wr_w_in", [P, H], I32)
+        wr_s_in = held("wr_s_in", [P, H // 4], I32)
+        wr_w = held("wr_w", [P, H], I32)
+        wr_s = held("wr_s", [P, H], U8)
+        wm_w = held("wm_w", [P, 2, N // 2], I32)
+        wm_s = held("wm_s", [P, 2, N // 4], I32)
+        b_sb = held("b_sb", [P, 2, PACK], F32)
+        gain_sb = held("gain_sb", [P, 2, PACK], F32)
+        bm_sb = held("bm_sb", [P, N // P], F32)
+        v_w = [held("v_w%d" % a, [P, S], U32) for a in range(2)]
+        v_s = held("v_s", [P, S], U8)
+        v2_w = held("v2_w", [P, S], U32)
+        v2_s = held("v2_s", [P, S], U8)
+        ws_raw = {(a, c): held("ws_raw%d%d" % (a, c), [P, PACK, KP], F32) for a in range(2) for c in range(2)}
+        ws_bf = {(a, c): held("ws_bf%d%d" % (a, c), [P, PACK * KP], BF16) for a in range(2) for c in range(2)}
+        ws_w = {(a, c): held("ws_w%d%d" % (a, c), [P, KP], U32) for a in range(2) for c in range(2)}
+        ws_s = {(a, c): held("ws_s%d%d" % (a, c), [P, KP], U8) for a in range(2) for c in range(2)}
+        h_w = {(c, g): held("h_w%d%d" % (c, g), [P, NJ], U32) for c in range(2) for g in range(2)}
+        h_s = {(c, g): held("h_s%d%d" % (c, g), [P, NJ], U8) for c in range(2) for g in range(2)}
+        warm = held("warm", [P, 2], F32)
+        banks = {(g, t): psum.tile([P, NJ], F32, name="bank%d%d" % (g, t)) for g in range(2) for t in range(PACK)}
+
+        nc.vector.memset(tab_s[:], 0)
+        nc.vector.memset(wr_s_in[:], 0)
+        nc.vector.memset(tab2_s[:], 0)
+        nc.vector.memset(wm_s[:], 0)
+        nc.vector.memset(warm[:, 0:1], 0.0)
+        nc.scalar.activation(warm[:, 1:2], warm[:, 0:1], ACT.Tanh)
+
+        def words(ap):
+            return ap.rearrange("p n i -> p (n i)").bitcast(I32)
+
+        def load_ws(a, c):
+            rows = ws[a * KP : (a + 1) * KP, c * KP : (c + 1) * KP]
+            nc.sync.dma_start(out=ws_raw[a, c][:], in_=rows.rearrange("(p j) r -> p j r", j=PACK))
+
+        for q in range(4):
+            nc.gpsimd.dma_start(out=tab_s[32 * q : 32 * q + 8, :], in_=tab_scales[:, 4 * q : 4 * q + 4, :].bitcast(I32))
+
+        nc.sync.dma_start(out=wr_w_in[:], in_=words(wr_words[0]))
+        nc.sync.dma_start(idx2[:], offs2)
+        nc.sync.dma_start(out=tab2_w[:], in_=words(tab2_words[0]))
+        nc.sync.dma_start(out=tab_w[0][:], in_=words(tab_words[0]))
+        wr_rows = wr_scales[0].rearrange("(q r) n -> r q n", r=4)
+        tab2_rows = tab2_scales[0].rearrange("(q r) n -> r q n", r=4)
+        for r in range(4):
+            nc.sync.dma_start(out=wr_s_in[WR_ROW + r : P : 32, :], in_=wr_rows[r].bitcast(I32))
+        for r in range(4):
+            nc.sync.dma_start(out=tab2_s[TAB2_ROW + r : P : 32, :], in_=tab2_rows[r].bitcast(I32))
+        nc.sync.dma_start(idx[:], offs)
+        load_ws(0, 0)
+        nc.sync.dma_start(out=b_sb[:], in_=b.rearrange("(c p t) -> p c t", p=P, t=PACK))
+        nc.sync.dma_start(out=gain_sb[:], in_=gain.rearrange("(c p t) -> p c t", p=P, t=PACK))
+        load_ws(1, 0)
+        nc.sync.dma_start(out=tab_w[1][:], in_=words(tab_words[1]))
+        load_ws(0, 1)
+        load_ws(1, 1)
+        nc.sync.dma_start(out=wm_w[:], in_=wm_words.rearrange("a p n -> p a n").bitcast(I32))
+        wm_rows = wm_scales.rearrange("a (q r) n -> r q a n", r=4)
+        for r in range(4):
+            nc.sync.dma_start(out=wm_s[r:P:32, :, :], in_=wm_rows[r].bitcast(I32))
+        with nc.allow_non_contiguous_dma(reason="one bias value a partition"):
+            nc.sync.dma_start(out=bm_sb[:], in_=bm.rearrange("(c p) -> p c", p=P))
+
+        def gather(dst, window, offsets, lo, hi):
+            nc.vector.tensor_copy(dst[:, lo:hi], window.indirect(offsets[:, lo // 16 : hi // 16]))
+
+        def regroup_ws(engine_copy, a, c, m0, m1):
+            dst = ws_bf[a, c][:].rearrange("p (t m j) -> p m j t", t=PACK, j=PACK)
+            src = ws_raw[a, c][:].rearrange("p j (m t) -> p m j t", t=PACK)
+            engine_copy(dst[:, m0:m1], src[:, m0:m1])
+
+        def quantise_ws(a, c):
+            nc.vector.quantize_mx(out=ws_w[a, c][:].bitcast(FP8X4), scales=ws_s[a, c][:], in_=ws_bf[a, c][:])
+
+        def pass_wr(c, g):
+            for t in range(PACK):
+                cols = slice(c * KP + t * P, c * KP + (t + 1) * P)
+                edges = slice(g * NJ, (g + 1) * NJ)
+                nc.tensor.matmul_mx(
+                    out=banks[g, t][:],
+                    lhsT=wr_w[:, cols].bitcast(FP8X4), lhsT_scale=wr_s[WR_ROW:P, cols],
+                    rhs=v2_w[:, edges].bitcast(FP8X4), rhs_scale=v2_s[TAB2_ROW:P, edges],
+                    start=True, stop=False,
+                )
+
+        def pass_ws(a, c, g):
+            for t in range(PACK):
+                cols = slice(t * P, (t + 1) * P)
+                edges = slice(g * NJ, (g + 1) * NJ)
+                nc.tensor.matmul_mx(
+                    out=banks[g, t][:],
+                    lhsT=ws_w[a, c][:, cols].bitcast(FP8X4), lhsT_scale=ws_s[a, c][:, cols],
+                    rhs=v_w[a][:, edges].bitcast(FP8X4), rhs_scale=v_s[4 * a : P, edges],
+                    start=False, stop=(a == 1),
+                )
+
+        act = {}
+
+        def tanh(c, g):
+            act[c, g] = ring.tile([P, PACK, NJ], F32, name="act")
+            for t in range(PACK):
+                nc.scalar.activation(act[c, g][:, t, :], banks[g, t][:], ACT.Tanh, bias=b_sb[:, c, t : t + 1])
+
+        def scale_and_quantise(c, g):
+            h_bf = ring.tile([P, PACK * NJ], BF16, name="h_bf", align_bytes=64)
+            dst = h_bf[:].rearrange("p (u i t) -> p u t i", i=4, t=PACK)
+            src = act[c, g][:].rearrange("p t (u i) -> p u t i", i=4)
+            half = NJ // 8
+            factor = gain_sb[:, c, :].unsqueeze(1).unsqueeze(3).broadcast_to([P, half, PACK, 4])
+            for u0 in (0, half):
+                nc.vector.tensor_tensor(dst[:, u0 : u0 + half], src[:, u0 : u0 + half], factor, ALU.mult)
+            nc.vector.quantize_mx(out=h_w[c, g][:].bitcast(FP8X4), scales=h_s[c, g][:], in_=h_bf[:])
+
+        def pass_wm(c, g):
+            for n in range(N // P):
+                nc.tensor.matmul_mx(
+                    out=banks[g, n][:],
+                    lhsT=wm_w[:, c, :].bitcast(U8)[:, 2 * n * P : 2 * (n + 1) * P].bitcast(FP4X4),
+                    lhsT_scale=wm_s[:, c, :].bitcast(U8)[:, n * P : (n + 1) * P],
+                    rhs=h_w[c, g][:].bitcast(FP8X4), rhs_scale=h_s[c, g][:],
+                    start=(c == 0), stop=(c == 1),
+                )
+
+        def emit(g, on_vector):
+            for n in range(N // P):
+                res = keep.tile([P, NJ], F32, name="res%d%d" % (g, n))
+                if n in on_vector:
+                    nc.vector.tensor_scalar(res[:], banks[g, n][:], bm_sb[:, n : n + 1], None, ALU.add)
+                else:
+                    nc.scalar.activation(res[:], banks[g, n][:], ACT.Identity, bias=bm_sb[:, n : n + 1])
+                nc.sync.dma_start(out=out[n * P : (n + 1) * P, g * NJ : (g + 1) * NJ], in_=res[:])
+
+        nc.vector.tensor_copy(
+            wr_w[:].rearrange("p (c t m) -> p c m t", c=2, t=PACK), wr_w_in[:].rearrange("p (c m t) -> p c m t", c=2, t=PACK)
+        )
+        gather(v2_w, tab2_w[:].bitcast(U32), idx2, 0, S)
+        gather(v2_s, tab2_s[:].bitcast(U8), idx2, 0, S)
+        nc.vector.tensor_copy(
+            wr_s[:].rearrange("p (c t m) -> p c m t", c=2, t=PACK),
+            wr_s_in[:].bitcast(U8).rearrange("p (c m t) -> p c m t", c=2, t=PACK),
+        )
+        for g in range(2):
+            pass_wr(0, g)
+        gather(v_w[0], tab_w[0][:].bitcast(U32), idx, 0, S)
+        gather(v_s, tab_s[:].bitcast(U8), idx, 0, S)
+        regroup_ws(nc.scalar.copy, 0, 0, 0, P)
+        quantise_ws(0, 0)
+        for g in range(2):
+            pass_ws(0, 0, g)
+        regroup_ws(nc.scalar.copy, 1, 0, 0, P)
+        quantise_ws(1, 0)
+
+        gather(v_w[1], tab_w[1][:].bitcast(U32), idx, 0, NJ)
+        pass_ws(1, 0, 0)
+        tanh(0, 0)
+        gather(v_w[1], tab_w[1][:].bitcast(U32), idx, NJ, S)
+        pass_ws(1, 0, 1)
+        regroup_ws(nc.vector.tensor_copy, 0, 1, 0, P)
+        quantise_ws(0, 1)
+        regroup_ws(nc.scalar.copy, 1, 1, 0, LAST_SCALAR_M)
+        regroup_ws(nc.vector.tensor_copy, 1, 1, LAST_SCALAR_M, P)
+        quantise_ws(1, 1)
+        tanh(0, 1)
+        for g in range(2):
+            pass_wr(1, g)
+            pass_ws(0, 1, g)
+            pass_ws(1, 1, g)
+            scale_and_quantise(0, g)
+            tanh(1, g)
+        for g in range(2):
+            pass_wm(0, g)
+            scale_and_quantise(1, g)
+            pass_wm(1, g)
+        emit(0, ())
+        emit(1, (1, 3))

@@ -67,8 +67,8 @@ def tile_list_bipartite_edge_messages_kernel(
         banks = {(g, t): psum.tile([P, NJ], F32, name="bank%d%d" % (g, t)) for g in range(2) for t in range(PACK)}
 
         nc.vector.memset(tab_s[:], 0)
-        nc.vector.memset(wr_s_in[:], 0)
         nc.vector.memset(tab2_s[:], 0)
+        nc.vector.memset(wr_s_in[:], 0)
         nc.vector.memset(wm_s[:], 0)
         nc.vector.memset(warm[:, 0:1], 0.0)
         nc.scalar.activation(warm[:, 1:2], warm[:, 0:1], ACT.Tanh)
@@ -114,7 +114,14 @@ def tile_list_bipartite_edge_messages_kernel(
         def regroup_ws(engine_copy, a, c, m0, m1):
             dst = ws_bf[a, c][:].rearrange("p (t m j) -> p m j t", t=PACK, j=PACK)
             src = ws_raw[a, c][:].rearrange("p j (m t) -> p m j t", t=PACK)
-            engine_copy(dst[:, m0:m1], src[:, m0:m1])
+            for t0 in (0, 2):
+                engine_copy(dst[:, m0:m1, :, t0 : t0 + 2], src[:, m0:m1, :, t0 : t0 + 2])
+
+        def permute_wr(dst, src):
+            dst = dst.rearrange("p (c t m) -> p c m t", c=2, t=PACK)
+            src = src.rearrange("p (c m t) -> p c m t", c=2, t=PACK)
+            for t0 in (0, 2):
+                nc.vector.tensor_copy(dst[:, :, :, t0 : t0 + 2], src[:, :, :, t0 : t0 + 2])
 
         def quantise_ws(a, c):
             nc.vector.quantize_mx(out=ws_w[a, c][:].bitcast(FP8X4), scales=ws_s[a, c][:], in_=ws_bf[a, c][:])
@@ -177,15 +184,10 @@ def tile_list_bipartite_edge_messages_kernel(
                     nc.scalar.activation(res[:], banks[g, n][:], ACT.Identity, bias=bm_sb[:, n : n + 1])
                 nc.sync.dma_start(out=out[n * P : (n + 1) * P, g * NJ : (g + 1) * NJ], in_=res[:])
 
-        nc.vector.tensor_copy(
-            wr_w[:].rearrange("p (c t m) -> p c m t", c=2, t=PACK), wr_w_in[:].rearrange("p (c m t) -> p c m t", c=2, t=PACK)
-        )
+        permute_wr(wr_w[:], wr_w_in[:])
         gather(v2_w, tab2_w[:].bitcast(U32), idx2, 0, S)
         gather(v2_s, tab2_s[:].bitcast(U8), idx2, 0, S)
-        nc.vector.tensor_copy(
-            wr_s[:].rearrange("p (c t m) -> p c m t", c=2, t=PACK),
-            wr_s_in[:].bitcast(U8).rearrange("p (c m t) -> p c m t", c=2, t=PACK),
-        )
+        permute_wr(wr_s[:], wr_s_in[:].bitcast(U8))
         for g in range(2):
             pass_wr(0, g)
         gather(v_w[0], tab_w[0][:].bitcast(U32), idx, 0, S)

@@ -1,3 +1,4 @@
+import math
 from contextlib import ExitStack
 
 import concourse.mybir as mybir
@@ -22,7 +23,8 @@ KP = P * PACK
 NJ = 512
 TAB2_ROW = 8
 WR_ROW = 12
-LAST_SCALAR_M = 40
+ON_GPSIMD = 2
+HELP = {(0, 1): 0, (1, 1): 0}
 
 
 def tile_list_bipartite_edge_messages_kernel(
@@ -32,7 +34,8 @@ def tile_list_bipartite_edge_messages_kernel(
     nc = tc.nc
     with ExitStack() as ctx:
         keep = ctx.enter_context(tc.tile_pool(name="keep", bufs=1))
-        ring = ctx.enter_context(tc.tile_pool(name="ring", bufs=3))
+        mid = ctx.enter_context(tc.tile_pool(name="mid", bufs=1))
+        late = ctx.enter_context(tc.tile_pool(name="late", bufs=1))
         psum = ctx.enter_context(tc.psum_pool(name="psum", bufs=1))
 
         def held(name, shape, dtype):
@@ -40,82 +43,35 @@ def tile_list_bipartite_edge_messages_kernel(
 
         idx = keep.tile([P, S // 16], U16, name="idx")
         idx2 = keep.tile([P, S // 16], U16, name="idx2")
-        tab_w = [held("tab_w%d" % a, [P, T], I32) for a in range(2)]
         tab_s = held("tab_s", [P, T // 4], I32)
         tab2_w = held("tab2_w", [P, T2], I32)
         tab2_s = held("tab2_s", [P, T2 // 4], I32)
-        wr_w_in = held("wr_w_in", [P, H], I32)
-        wr_s_in = held("wr_s_in", [P, H // 4], I32)
         wr_w = held("wr_w", [P, H], I32)
         wr_s = held("wr_s", [P, H], U8)
-        wm_w = held("wm_w", [P, 2, N // 2], I32)
-        wm_s = held("wm_s", [P, 2, N // 4], I32)
-        b_sb = held("b_sb", [P, 2, PACK], F32)
-        gain_sb = held("gain_sb", [P, 2, PACK], F32)
-        bm_sb = held("bm_sb", [P, N // P], F32)
         v_w = [held("v_w%d" % a, [P, S], U32) for a in range(2)]
-        v_s = held("v_s", [P, S], U8)
         v2_w = held("v2_w", [P, S], U32)
         v2_s = held("v2_s", [P, S], U8)
-        ws_raw = {(a, c): held("ws_raw%d%d" % (a, c), [P, PACK, KP], F32) for a in range(2) for c in range(2)}
-        ws_bf = {(a, c): held("ws_bf%d%d" % (a, c), [P, PACK * KP], BF16) for a in range(2) for c in range(2)}
-        ws_w = {(a, c): held("ws_w%d%d" % (a, c), [P, KP], U32) for a in range(2) for c in range(2)}
-        ws_s = {(a, c): held("ws_s%d%d" % (a, c), [P, KP], U8) for a in range(2) for c in range(2)}
-        h_w = {(c, g): held("h_w%d%d" % (c, g), [P, NJ], U32) for c in range(2) for g in range(2)}
-        h_s = {(c, g): held("h_s%d%d" % (c, g), [P, NJ], U8) for c in range(2) for g in range(2)}
-        warm = held("warm", [P, 2], F32)
+        pieces = [(a, c, u) for a in range(2) for c in range(2) for u in range(2)]
+        ws_bf = {k: held("ws_bf%d%d%d" % k, [P, 2 * KP], BF16) for k in pieces}
+        ws_w = {k: held("ws_w%d%d%d" % k, [P, 2 * P], U32) for k in pieces}
+        ws_s = {k: held("ws_s%d%d%d" % k, [P, 2 * P], U8) for k in pieces}
+        chunks = [(c, g) for c in range(2) for g in range(2)]
+        act = {k: held("act%d%d" % k, [P, PACK, NJ], F32) for k in chunks}
+        h_bf = {k: held("h_bf%d%d" % k, [P, PACK * NJ], BF16) for k in chunks}
+        h_w = {k: held("h_w%d%d" % k, [P, NJ], U32) for k in chunks}
+        h_s = {k: held("h_s%d%d" % k, [P, NJ], U8) for k in chunks}
         banks = {(g, t): psum.tile([P, NJ], F32, name="bank%d%d" % (g, t)) for g in range(2) for t in range(PACK)}
 
-        nc.vector.memset(tab_s[:], 0)
-        nc.vector.memset(tab2_s[:], 0)
-        nc.vector.memset(wr_s_in[:], 0)
-        nc.vector.memset(wm_s[:], 0)
-        nc.vector.memset(warm[:, 0:1], 0.0)
-        nc.scalar.activation(warm[:, 1:2], warm[:, 0:1], ACT.Tanh)
+        later = [("ws_raw%d%d" % (a, c), [P, PACK, KP], F32) for c in range(2) for a in range(2)] + [
+            ("tab_w1", [P, T], I32), ("wm_w", [P, 2, N // 2], I32), ("wm_s", [P, 2, N // 4], I32), ("b_sb", [P, 2, PACK], F32), ("gain_sb", [P, 2, PACK], F32),
+            ("bm_sb", [P, N // P], F32),
+        ]
+        sizes = [64 * ((4 * math.prod(shape[1:]) + 63) // 64) for name, shape, dtype in later]
+        staged = late.tile([P, sum(sizes) // 4], I32, name="staged", offset=0, align_bytes=64)
+        warm = mid.tile([P, T + H // 4], F32, name="warm", offset=0, align_bytes=64)
 
         def words(ap):
             return ap.rearrange("p n i -> p (n i)").bitcast(I32)
-
-        def load_ws(a, c):
-            rows = ws[a * KP : (a + 1) * KP, c * KP : (c + 1) * KP]
-            nc.sync.dma_start(out=ws_raw[a, c][:], in_=rows.rearrange("(p j) r -> p j r", j=PACK))
-
-        for q in range(4):
-            nc.gpsimd.dma_start(out=tab_s[32 * q : 32 * q + 8, :], in_=tab_scales[:, 4 * q : 4 * q + 4, :].bitcast(I32))
-
-        nc.sync.dma_start(out=wr_w_in[:], in_=words(wr_words[0]))
-        nc.sync.dma_start(idx2[:], offs2)
-        nc.sync.dma_start(out=tab2_w[:], in_=words(tab2_words[0]))
-        nc.sync.dma_start(out=tab_w[0][:], in_=words(tab_words[0]))
-        wr_rows = wr_scales[0].rearrange("(q r) n -> r q n", r=4)
-        tab2_rows = tab2_scales[0].rearrange("(q r) n -> r q n", r=4)
-        for r in range(4):
-            nc.sync.dma_start(out=wr_s_in[WR_ROW + r : P : 32, :], in_=wr_rows[r].bitcast(I32))
-        for r in range(4):
-            nc.sync.dma_start(out=tab2_s[TAB2_ROW + r : P : 32, :], in_=tab2_rows[r].bitcast(I32))
-        nc.sync.dma_start(idx[:], offs)
-        load_ws(0, 0)
-        nc.sync.dma_start(out=b_sb[:], in_=b.rearrange("(c p t) -> p c t", p=P, t=PACK))
-        nc.sync.dma_start(out=gain_sb[:], in_=gain.rearrange("(c p t) -> p c t", p=P, t=PACK))
-        load_ws(1, 0)
-        nc.sync.dma_start(out=tab_w[1][:], in_=words(tab_words[1]))
-        load_ws(0, 1)
-        load_ws(1, 1)
-        nc.sync.dma_start(out=wm_w[:], in_=wm_words.rearrange("a p n -> p a n").bitcast(I32))
-        wm_rows = wm_scales.rearrange("a (q r) n -> r q a n", r=4)
-        for r in range(4):
-            nc.sync.dma_start(out=wm_s[r:P:32, :, :], in_=wm_rows[r].bitcast(I32))
-        with nc.allow_non_contiguous_dma(reason="one bias value a partition"):
-            nc.sync.dma_start(out=bm_sb[:], in_=bm.rearrange("(c p) -> p c", p=P))
-
-        def gather(dst, window, offsets, lo, hi):
-            nc.vector.tensor_copy(dst[:, lo:hi], window.indirect(offsets[:, lo // 16 : hi // 16]))
-
-        def regroup_ws(engine_copy, a, c, m0, m1):
-            dst = ws_bf[a, c][:].rearrange("p (t m j) -> p m j t", t=PACK, j=PACK)
-            src = ws_raw[a, c][:].rearrange("p j (m t) -> p m j t", t=PACK)
-            for t0 in (0, 2):
-                engine_copy(dst[:, m0:m1, :, t0 : t0 + 2], src[:, m0:m1, :, t0 : t0 + 2])
 
         def permute_wr(dst, src):
             dst = dst.rearrange("p (c t m) -> p c m t", c=2, t=PACK)
@@ -123,47 +79,124 @@ def tile_list_bipartite_edge_messages_kernel(
             for t0 in (0, 2):
                 nc.vector.tensor_copy(dst[:, :, :, t0 : t0 + 2], src[:, :, :, t0 : t0 + 2])
 
-        def quantise_ws(a, c):
-            nc.vector.quantize_mx(out=ws_w[a, c][:].bitcast(FP8X4), scales=ws_s[a, c][:], in_=ws_bf[a, c][:])
+        nc.vector.memset(warm[:, T : T + 1], 0.0)
+        nc.gpsimd.memset(tab_s[:], 0)
+        nc.vector.memset(tab2_s[:], 0)
+        nc.scalar.activation(warm[:, T + 1 : T + 2], warm[:, T : T + 1], ACT.Tanh)
 
-        def pass_wr(c, g):
+        nc.sync.dma_start(idx2[:], offs2)
+        nc.sync.dma_start(idx[:], offs)
+        nc.sync.dma_start(out=staged[:, 0:H], in_=words(wr_words[0]))
+        nc.sync.dma_start(out=tab2_w[:], in_=words(tab2_words[0]))
+        wr_rows = wr_scales[0].rearrange("(q r) n -> r q n", r=4)
+        tab2_rows = tab2_scales[0].rearrange("(q r) n -> r q n", r=4)
+        for r in range(4):
+            nc.sync.dma_start(out=tab2_s[TAB2_ROW + r : P : 32, :], in_=tab2_rows[r].bitcast(I32))
+        for q in range(4):
+            queue = nc.gpsimd if q < ON_GPSIMD else nc.sync
+            queue.dma_start(out=tab_s[32 * q : 32 * q + 8, :], in_=tab_scales[:, 4 * q : 4 * q + 4, :].bitcast(I32))
+
+        tab_w0 = mid.tile([P, T], I32, name="tab_w0", offset=0, align_bytes=64)
+        wr_s_in = mid.tile([P, H // 4], I32, name="wr_s_in", offset=4 * T, align_bytes=64)
+        nc.vector.memset(wr_s_in[:], 0)
+        nc.sync.dma_start(out=tab_w0[:], in_=words(tab_words[0]))
+        for r in range(4):
+            nc.sync.dma_start(out=wr_s_in[WR_ROW + r : P : 32, :], in_=wr_rows[r].bitcast(I32))
+        permute_wr(wr_w[:], staged[:, 0:H])
+
+        placed = {
+            name: late.tile(shape, dtype, name=name, offset=sum(sizes[:i]), align_bytes=64)
+            for i, (name, shape, dtype) in enumerate(later)
+        }
+        ws_raw = {(a, c): placed["ws_raw%d%d" % (a, c)] for a in range(2) for c in range(2)}
+        tab_w = [tab_w0, placed["tab_w1"]]
+        wm_w, wm_s = placed["wm_w"], placed["wm_s"]
+        b_sb, gain_sb, bm_sb = placed["b_sb"], placed["gain_sb"], placed["bm_sb"]
+        nc.vector.memset(wm_s[:], 0)
+
+        def load_ws(a, c):
+            rows = ws[a * KP : (a + 1) * KP, c * KP : (c + 1) * KP]
+            nc.sync.dma_start(out=ws_raw[a, c][:], in_=rows.rearrange("(p j) r -> p j r", j=PACK))
+
+        load_ws(0, 0)
+        nc.sync.dma_start(out=b_sb[:], in_=b.rearrange("(c p t) -> p c t", p=P, t=PACK))
+        nc.sync.dma_start(out=tab_w[1][:], in_=words(tab_words[1]))
+        nc.sync.dma_start(out=gain_sb[:], in_=gain.rearrange("(c p t) -> p c t", p=P, t=PACK))
+        load_ws(1, 0)
+        load_ws(0, 1)
+        load_ws(1, 1)
+        nc.sync.dma_start(out=wm_w[:], in_=wm_words.rearrange("a p n -> p a n").bitcast(I32))
+        with nc.allow_non_contiguous_dma(reason="one bias value a partition"):
+            nc.sync.dma_start(out=bm_sb[:], in_=bm.rearrange("(c p) -> p c", p=P))
+        wm_rows = wm_scales.rearrange("a (q r) n -> r q a n", r=4)
+        for r in range(4):
+            nc.sync.dma_start(out=wm_s[r:P:32, :, :], in_=wm_rows[r].bitcast(I32))
+
+        def gather(dst, window, offsets):
+            nc.vector.tensor_copy(dst[:], window.indirect(offsets[:]))
+
+        def regroup_ws(engine_copy, a, c, u):
+            dst = ws_bf[a, c, u][:].rearrange("p (t m j) -> p m j t", t=2, j=PACK)
+            src = ws_raw[a, c][:].rearrange("p j (m t) -> p m j t", t=PACK)
+            engine_copy(dst, src[:, :, :, 2 * u : 2 * u + 2])
+
+        def quantise_ws(a, c, u):
+            nc.vector.quantize_mx(out=ws_w[a, c, u][:].bitcast(FP8X4), scales=ws_s[a, c, u][:], in_=ws_bf[a, c, u][:])
+
+        def prepare_ws(a, c, copies):
+            for u in range(2):
+                regroup_ws(copies[u], a, c, u)
+            for u in range(2):
+                quantise_ws(a, c, u)
+
+        def pass_wr(c, g, t):
+            cols = slice(c * KP + t * P, c * KP + (t + 1) * P)
+            edges = slice(g * NJ, (g + 1) * NJ)
+            nc.tensor.matmul_mx(
+                out=banks[g, t][:],
+                lhsT=wr_w[:, cols].bitcast(FP8X4), lhsT_scale=wr_s[WR_ROW:P, cols],
+                rhs=v2_w[:, edges].bitcast(FP8X4), rhs_scale=v2_s[TAB2_ROW:P, edges],
+                start=True, stop=False,
+            )
+
+        def pass_ws(a, c, g, t):
+            cols = slice(t % 2 * P, (t % 2 + 1) * P)
+            edges = slice(g * NJ, (g + 1) * NJ)
+            nc.tensor.matmul_mx(
+                out=banks[g, t][:],
+                lhsT=ws_w[a, c, t // 2][:, cols].bitcast(FP8X4), lhsT_scale=ws_s[a, c, t // 2][:, cols],
+                rhs=v_w[a][:, edges].bitcast(FP8X4), rhs_scale=v_s[4 * a : P, edges],
+                start=False, stop=(a == 1),
+            )
+
+        def tanh(c, g, t):
+            nc.scalar.activation(act[c, g][:, t, :], banks[g, t][:], ACT.Tanh, bias=b_sb[:, c, t : t + 1])
+
+        def scale_on_scalar(c, g):
+            e0 = NJ - HELP.get((c, g), 0)
+            if e0 == NJ:
+                return
+            planes = held("planes%d%d" % (c, g), [P, PACK, NJ - e0], BF16)
             for t in range(PACK):
-                cols = slice(c * KP + t * P, c * KP + (t + 1) * P)
-                edges = slice(g * NJ, (g + 1) * NJ)
-                nc.tensor.matmul_mx(
-                    out=banks[g, t][:],
-                    lhsT=wr_w[:, cols].bitcast(FP8X4), lhsT_scale=wr_s[WR_ROW:P, cols],
-                    rhs=v2_w[:, edges].bitcast(FP8X4), rhs_scale=v2_s[TAB2_ROW:P, edges],
-                    start=True, stop=False,
-                )
-
-        def pass_ws(a, c, g):
-            for t in range(PACK):
-                cols = slice(t * P, (t + 1) * P)
-                edges = slice(g * NJ, (g + 1) * NJ)
-                nc.tensor.matmul_mx(
-                    out=banks[g, t][:],
-                    lhsT=ws_w[a, c][:, cols].bitcast(FP8X4), lhsT_scale=ws_s[a, c][:, cols],
-                    rhs=v_w[a][:, edges].bitcast(FP8X4), rhs_scale=v_s[4 * a : P, edges],
-                    start=False, stop=(a == 1),
-                )
-
-        act = {}
-
-        def tanh(c, g):
-            act[c, g] = ring.tile([P, PACK, NJ], F32, name="act")
-            for t in range(PACK):
-                nc.scalar.activation(act[c, g][:, t, :], banks[g, t][:], ACT.Tanh, bias=b_sb[:, c, t : t + 1])
+                nc.scalar.activation(planes[:, t, :], act[c, g][:, t, e0:NJ], ACT.Copy, scale=gain_sb[:, c, t : t + 1])
+            dst = h_bf[c, g][:, PACK * e0 : PACK * NJ].rearrange("p (u i t) -> p u t i", i=4, t=PACK)
+            nc.scalar.copy(dst, planes[:].rearrange("p t (u i) -> p u t i", i=4))
 
         def scale_and_quantise(c, g):
-            h_bf = ring.tile([P, PACK * NJ], BF16, name="h_bf", align_bytes=64)
-            dst = h_bf[:].rearrange("p (u i t) -> p u t i", i=4, t=PACK)
+            dst = h_bf[c, g][:].rearrange("p (u i t) -> p u t i", i=4, t=PACK)
             src = act[c, g][:].rearrange("p t (u i) -> p u t i", i=4)
             half = NJ // 8
-            factor = gain_sb[:, c, :].unsqueeze(1).unsqueeze(3).broadcast_to([P, half, PACK, 4])
-            for u0 in (0, half):
-                nc.vector.tensor_tensor(dst[:, u0 : u0 + half], src[:, u0 : u0 + half], factor, ALU.mult)
-            nc.vector.quantize_mx(out=h_w[c, g][:].bitcast(FP8X4), scales=h_s[c, g][:], in_=h_bf[:])
+            end = (NJ - HELP.get((c, g), 0)) // 4
+            for u0, u1 in ((0, min(half, end)), (half, end)):
+                if u1 > u0:
+                    factor = gain_sb[:, c, :].unsqueeze(1).unsqueeze(3).broadcast_to([P, u1 - u0, PACK, 4])
+                    nc.vector.tensor_tensor(dst[:, u0:u1], src[:, u0:u1], factor, ALU.mult)
+            for e0 in (0, NJ // 2):
+                cols = slice(e0, e0 + NJ // 2)
+                nc.vector.quantize_mx(
+                    out=h_w[c, g][:, cols].bitcast(FP8X4), scales=h_s[c, g][:, cols],
+                    in_=h_bf[c, g][:, PACK * e0 : PACK * (e0 + NJ // 2)],
+                )
 
         def pass_wm(c, g):
             for n in range(N // P):
@@ -184,41 +217,43 @@ def tile_list_bipartite_edge_messages_kernel(
                     nc.scalar.activation(res[:], banks[g, n][:], ACT.Identity, bias=bm_sb[:, n : n + 1])
                 nc.sync.dma_start(out=out[n * P : (n + 1) * P, g * NJ : (g + 1) * NJ], in_=res[:])
 
-        permute_wr(wr_w[:], wr_w_in[:])
-        gather(v2_w, tab2_w[:].bitcast(U32), idx2, 0, S)
-        gather(v2_s, tab2_s[:].bitcast(U8), idx2, 0, S)
+        on_scalar, on_vector = nc.scalar.copy, nc.vector.tensor_copy
+        gather(v2_w, tab2_w[:].bitcast(U32), idx2)
+        gather(v2_s, tab2_s[:].bitcast(U8), idx2)
         permute_wr(wr_s[:], wr_s_in[:].bitcast(U8))
+        gather(v_w[0], tab_w[0][:].bitcast(U32), idx)
+        v_s = mid.tile([P, S], U8, name="v_s", offset=4 * T, align_bytes=64)
+        gather(v_s, tab_s[:].bitcast(U8), idx)
         for g in range(2):
-            pass_wr(0, g)
-        gather(v_w[0], tab_w[0][:].bitcast(U32), idx, 0, S)
-        gather(v_s, tab_s[:].bitcast(U8), idx, 0, S)
-        regroup_ws(nc.scalar.copy, 0, 0, 0, P)
-        quantise_ws(0, 0)
+            for t in range(PACK):
+                pass_wr(0, g, t)
+        prepare_ws(0, 0, (on_scalar, on_scalar))
         for g in range(2):
-            pass_ws(0, 0, g)
-        regroup_ws(nc.scalar.copy, 1, 0, 0, P)
-        quantise_ws(1, 0)
-
-        gather(v_w[1], tab_w[1][:].bitcast(U32), idx, 0, NJ)
-        pass_ws(1, 0, 0)
-        tanh(0, 0)
-        gather(v_w[1], tab_w[1][:].bitcast(U32), idx, NJ, S)
-        pass_ws(1, 0, 1)
-        regroup_ws(nc.vector.tensor_copy, 0, 1, 0, P)
-        quantise_ws(0, 1)
-        regroup_ws(nc.scalar.copy, 1, 1, 0, LAST_SCALAR_M)
-        regroup_ws(nc.vector.tensor_copy, 1, 1, LAST_SCALAR_M, P)
-        quantise_ws(1, 1)
-        tanh(0, 1)
+            for t in range(PACK):
+                pass_ws(0, 0, g, t)
+        gather(v_w[1], tab_w[1][:].bitcast(U32), idx)
+        prepare_ws(1, 0, (on_vector, on_scalar))
         for g in range(2):
-            pass_wr(1, g)
-            pass_ws(0, 1, g)
-            pass_ws(1, 1, g)
-            scale_and_quantise(0, g)
-            tanh(1, g)
+            for t in range(PACK):
+                pass_ws(1, 0, g, t)
+                tanh(0, g, t)
+        prepare_ws(0, 1, (on_vector, on_vector))
+        prepare_ws(1, 1, (on_vector, on_vector))
         for g in range(2):
-            pass_wm(0, g)
-            scale_and_quantise(1, g)
-            pass_wm(1, g)
+            for t in range(PACK):
+                pass_wr(1, g, t)
+                pass_ws(0, 1, g, t)
+                pass_ws(1, 1, g, t)
+                tanh(1, g, t)
+        scale_and_quantise(0, 0)
+        scale_and_quantise(1, 0)
+        scale_on_scalar(0, 1)
+        pass_wm(0, 0)
+        pass_wm(1, 0)
         emit(0, ())
+        scale_on_scalar(1, 1)
+        scale_and_quantise(0, 1)
+        pass_wm(0, 1)
+        scale_and_quantise(1, 1)
+        pass_wm(1, 1)
         emit(1, (1, 3))

@@ -23,8 +23,9 @@ KP = P * PACK
 NJ = 512
 TAB2_ROW = 8
 WR_ROW = 12
-ON_GPSIMD = 2
-HELP = {(0, 1): 0, (1, 1): 0}
+ON_GPSIMD = 4
+RUN = 2
+TAIL = ((0, 128), (128, 256), (384, 128))
 
 
 def tile_list_bipartite_edge_messages_kernel(
@@ -56,14 +57,14 @@ def tile_list_bipartite_edge_messages_kernel(
         ws_w = {k: held("ws_w%d%d%d" % k, [P, 2 * P], U32) for k in pieces}
         ws_s = {k: held("ws_s%d%d%d" % k, [P, 2 * P], U8) for k in pieces}
         chunks = [(c, g) for c in range(2) for g in range(2)]
-        act = {k: held("act%d%d" % k, [P, PACK, NJ], F32) for k in chunks}
-        h_bf = {k: held("h_bf%d%d" % k, [P, PACK * NJ], BF16) for k in chunks}
+        act = {k: keep.tile([P, PACK, NJ], F32, name="act%d%d" % k, tag="act%d%d" % k, align_bytes=64) for k in chunks}
+        h_bf = {k: held("h_bf%d%d" % k, [P, PACK * NJ], BF16) for k in chunks if k != (0, 1)}
         h_w = {k: held("h_w%d%d" % k, [P, NJ], U32) for k in chunks}
         h_s = {k: held("h_s%d%d" % k, [P, NJ], U8) for k in chunks}
         banks = {(g, t): psum.tile([P, NJ], F32, name="bank%d%d" % (g, t)) for g in range(2) for t in range(PACK)}
 
         later = [("ws_raw%d%d" % (a, c), [P, PACK, KP], F32) for c in range(2) for a in range(2)] + [
-            ("tab_w1", [P, T], I32), ("wm_w", [P, 2, N // 2], I32), ("wm_s", [P, 2, N // 4], I32), ("b_sb", [P, 2, PACK], F32), ("gain_sb", [P, 2, PACK], F32),
+            ("tab_w1", [P, T], I32), ("wm_w", [P, 2, N // 2], I32), ("wm_s", [P, 2, N // 4], I32), ("gain_sb", [P, 2, PACK], F32), ("b_sb", [P, 2, PACK], F32),
             ("bm_sb", [P, N // P], F32),
         ]
         sizes = [64 * ((4 * math.prod(shape[1:]) + 63) // 64) for name, shape, dtype in later]
@@ -85,9 +86,9 @@ def tile_list_bipartite_edge_messages_kernel(
         nc.scalar.activation(warm[:, T + 1 : T + 2], warm[:, T : T + 1], ACT.Tanh)
 
         nc.sync.dma_start(idx2[:], offs2)
-        nc.sync.dma_start(idx[:], offs)
         nc.sync.dma_start(out=staged[:, 0:H], in_=words(wr_words[0]))
         nc.sync.dma_start(out=tab2_w[:], in_=words(tab2_words[0]))
+        nc.sync.dma_start(idx[:], offs)
         wr_rows = wr_scales[0].rearrange("(q r) n -> r q n", r=4)
         tab2_rows = tab2_scales[0].rearrange("(q r) n -> r q n", r=4)
         for r in range(4):
@@ -108,23 +109,24 @@ def tile_list_bipartite_edge_messages_kernel(
             name: late.tile(shape, dtype, name=name, offset=sum(sizes[:i]), align_bytes=64)
             for i, (name, shape, dtype) in enumerate(later)
         }
-        ws_raw = {(a, c): placed["ws_raw%d%d" % (a, c)] for a in range(2) for c in range(2)}
+        ws_raw = {(a, c): placed["ws_raw%d%d" % (a, c)][:] for a in range(2) for c in range(2)}
         tab_w = [tab_w0, placed["tab_w1"]]
         wm_w, wm_s = placed["wm_w"], placed["wm_s"]
         b_sb, gain_sb, bm_sb = placed["b_sb"], placed["gain_sb"], placed["bm_sb"]
         nc.vector.memset(wm_s[:], 0)
 
+        ws_rows = ws.rearrange("(a p j) r -> a p j r", a=2, j=PACK)
+
         def load_ws(a, c):
-            rows = ws[a * KP : (a + 1) * KP, c * KP : (c + 1) * KP]
-            nc.sync.dma_start(out=ws_raw[a, c][:], in_=rows.rearrange("(p j) r -> p j r", j=PACK))
+            nc.sync.dma_start(out=ws_raw[a, c], in_=ws_rows[a][:, :, c * KP : (c + 1) * KP])
 
         load_ws(0, 0)
-        nc.sync.dma_start(out=b_sb[:], in_=b.rearrange("(c p t) -> p c t", p=P, t=PACK))
         nc.sync.dma_start(out=tab_w[1][:], in_=words(tab_words[1]))
-        nc.sync.dma_start(out=gain_sb[:], in_=gain.rearrange("(c p t) -> p c t", p=P, t=PACK))
         load_ws(1, 0)
+        nc.sync.dma_start(out=b_sb[:], in_=b.rearrange("(c p t) -> p c t", p=P, t=PACK))
         load_ws(0, 1)
         load_ws(1, 1)
+        nc.sync.dma_start(out=gain_sb[:], in_=gain.rearrange("(c p t) -> p c t", p=P, t=PACK))
         nc.sync.dma_start(out=wm_w[:], in_=wm_words.rearrange("a p n -> p a n").bitcast(I32))
         with nc.allow_non_contiguous_dma(reason="one bias value a partition"):
             nc.sync.dma_start(out=bm_sb[:], in_=bm.rearrange("(c p) -> p c", p=P))
@@ -137,7 +139,7 @@ def tile_list_bipartite_edge_messages_kernel(
 
         def regroup_ws(engine_copy, a, c, u):
             dst = ws_bf[a, c, u][:].rearrange("p (t m j) -> p m j t", t=2, j=PACK)
-            src = ws_raw[a, c][:].rearrange("p j (m t) -> p m j t", t=PACK)
+            src = ws_raw[a, c].rearrange("p j (m t) -> p m j t", t=PACK)
             engine_copy(dst, src[:, :, :, 2 * u : 2 * u + 2])
 
         def quantise_ws(a, c, u):
@@ -149,78 +151,100 @@ def tile_list_bipartite_edge_messages_kernel(
             for u in range(2):
                 quantise_ws(a, c, u)
 
-        def pass_wr(c, g, t):
+        def pass_wr(c, g, t, start=True):
             cols = slice(c * KP + t * P, c * KP + (t + 1) * P)
             edges = slice(g * NJ, (g + 1) * NJ)
             nc.tensor.matmul_mx(
                 out=banks[g, t][:],
                 lhsT=wr_w[:, cols].bitcast(FP8X4), lhsT_scale=wr_s[WR_ROW:P, cols],
                 rhs=v2_w[:, edges].bitcast(FP8X4), rhs_scale=v2_s[TAB2_ROW:P, edges],
-                start=True, stop=False,
+                start=start, stop=False,
             )
 
-        def pass_ws(a, c, g, t):
+        def pass_ws(a, c, g, t, turned=False):
             cols = slice(t % 2 * P, (t % 2 + 1) * P)
             edges = slice(g * NJ, (g + 1) * NJ)
             nc.tensor.matmul_mx(
                 out=banks[g, t][:],
                 lhsT=ws_w[a, c, t // 2][:, cols].bitcast(FP8X4), lhsT_scale=ws_s[a, c, t // 2][:, cols],
                 rhs=v_w[a][:, edges].bitcast(FP8X4), rhs_scale=v_s[4 * a : P, edges],
-                start=False, stop=(a == 1),
+                start=(turned and a == 1), stop=(a == (0 if turned else 1)),
             )
 
         def tanh(c, g, t):
             nc.scalar.activation(act[c, g][:, t, :], banks[g, t][:], ACT.Tanh, bias=b_sb[:, c, t : t + 1])
 
-        def scale_on_scalar(c, g):
-            e0 = NJ - HELP.get((c, g), 0)
-            if e0 == NJ:
-                return
-            planes = held("planes%d%d" % (c, g), [P, PACK, NJ - e0], BF16)
+        def scale(c, g, e0, width):
+            dst = h_bf[c, g][:, PACK * e0 : PACK * (e0 + width)].rearrange("p (u i t) -> p u t i", i=RUN, t=PACK)
+            src = act[c, g][:, :, e0 : e0 + width].rearrange("p t (u i) -> p u t i", i=RUN)
+            factor = gain_sb[:, c, :].unsqueeze(1).unsqueeze(3).broadcast_to([P, width // RUN, PACK, RUN])
+            nc.vector.tensor_tensor(dst, src, factor, ALU.mult)
+
+        def scale_on_scalar(c, g, e0, width):
+            planes = held("planes", [P, PACK, width], BF16)
             for t in range(PACK):
-                nc.scalar.activation(planes[:, t, :], act[c, g][:, t, e0:NJ], ACT.Copy, scale=gain_sb[:, c, t : t + 1])
-            dst = h_bf[c, g][:, PACK * e0 : PACK * NJ].rearrange("p (u i t) -> p u t i", i=4, t=PACK)
+                nc.scalar.activation(
+                    planes[:, t, :], act[c, g][:, t, e0 : e0 + width], ACT.Copy, scale=gain_sb[:, c, t : t + 1]
+                )
+            dst = h_bf[c, g][:, PACK * e0 : PACK * (e0 + width)].rearrange("p (u i t) -> p u t i", i=4, t=PACK)
             nc.scalar.copy(dst, planes[:].rearrange("p t (u i) -> p u t i", i=4))
 
-        def scale_and_quantise(c, g):
-            dst = h_bf[c, g][:].rearrange("p (u i t) -> p u t i", i=4, t=PACK)
-            src = act[c, g][:].rearrange("p t (u i) -> p u t i", i=4)
-            half = NJ // 8
-            end = (NJ - HELP.get((c, g), 0)) // 4
-            for u0, u1 in ((0, min(half, end)), (half, end)):
-                if u1 > u0:
-                    factor = gain_sb[:, c, :].unsqueeze(1).unsqueeze(3).broadcast_to([P, u1 - u0, PACK, 4])
-                    nc.vector.tensor_tensor(dst[:, u0:u1], src[:, u0:u1], factor, ALU.mult)
-            for e0 in (0, NJ // 2):
-                cols = slice(e0, e0 + NJ // 2)
-                nc.vector.quantize_mx(
-                    out=h_w[c, g][:, cols].bitcast(FP8X4), scales=h_s[c, g][:, cols],
-                    in_=h_bf[c, g][:, PACK * e0 : PACK * (e0 + NJ // 2)],
-                )
+        def quantise_h(c, g, e0, width):
+            cols = slice(e0, e0 + width)
+            nc.vector.quantize_mx(
+                out=h_w[c, g][:, cols].bitcast(FP8X4), scales=h_s[c, g][:, cols],
+                in_=h_bf[c, g][:, PACK * e0 : PACK * (e0 + width)],
+            )
 
-        def pass_wm(c, g):
-            for n in range(N // P):
-                nc.tensor.matmul_mx(
-                    out=banks[g, n][:],
-                    lhsT=wm_w[:, c, :].bitcast(U8)[:, 2 * n * P : 2 * (n + 1) * P].bitcast(FP4X4),
-                    lhsT_scale=wm_s[:, c, :].bitcast(U8)[:, n * P : (n + 1) * P],
-                    rhs=h_w[c, g][:].bitcast(FP8X4), rhs_scale=h_s[c, g][:],
-                    start=(c == 0), stop=(c == 1),
-                )
+        def scale_and_quantise(c, g, parts):
+            for i, part in enumerate(parts):
+                scale(c, g, *part)
+                if i > 0:
+                    quantise_h(c, g, *parts[i - 1])
+            quantise_h(c, g, *parts[-1])
 
-        def emit(g, on_vector):
-            for n in range(N // P):
-                res = keep.tile([P, NJ], F32, name="res%d%d" % (g, n))
-                if n in on_vector:
-                    nc.vector.tensor_scalar(res[:], banks[g, n][:], bm_sb[:, n : n + 1], None, ALU.add)
-                else:
-                    nc.scalar.activation(res[:], banks[g, n][:], ACT.Identity, bias=bm_sb[:, n : n + 1])
-                nc.sync.dma_start(out=out[n * P : (n + 1) * P, g * NJ : (g + 1) * NJ], in_=res[:])
+        def pass_wm(dst, c, g, n, e0, width, start, stop):
+            nc.tensor.matmul_mx(
+                out=dst,
+                lhsT=wm_w[:, c, :].bitcast(U8)[:, 2 * n * P : 2 * (n + 1) * P].bitcast(FP4X4),
+                lhsT_scale=wm_s[:, c, :].bitcast(U8)[:, n * P : (n + 1) * P],
+                rhs=h_w[c, g][:, e0 : e0 + width].bitcast(FP8X4), rhs_scale=h_s[c, g][:, e0 : e0 + width],
+                start=start, stop=stop,
+            )
+
+        out_rows = out.rearrange("(n p) e -> p n e", p=P)
+
+        def emit(bank, n0, count, e0, width, on_vector):
+            res = keep.tile([P, count, width], F32, name="res%d_%d" % (n0, e0))
+            sums = bank[:, 0 : count * width].rearrange("p (n e) -> p n e", n=count)
+            if on_vector:
+                shift = bm_sb[:, n0 : n0 + count].unsqueeze(2).broadcast_to([P, count, width])
+                nc.vector.tensor_tensor(res[:], sums, shift, ALU.add)
+            else:
+                for i in range(count):
+                    nc.scalar.activation(res[:, i, :], sums[:, i, :], ACT.Identity, bias=bm_sb[:, n0 + i : n0 + i + 1])
+            nc.sync.dma_start(out=out_rows[:, n0 : n0 + count, e0 : e0 + width], in_=res[:])
+
+        tail_banks = []
+        spare = [banks[1, t] for t in range(PACK)] + [banks[0, 0]]
+        for e0, width in TAIL:
+            count = NJ // width if e0 + width < NJ else 2
+            for n0 in range(0, N // P, count):
+                tail_banks.append((spare[len(tail_banks)], n0, count, e0, width))
+
+        def tail_passes(c, bank, n0, count, e0, width):
+            steps = [(i, d) for i in range(count) for d in range(0, width, P)]
+            for i, d in steps:
+                dst = bank[:, i * width + d : i * width + d + P]
+                pass_wm(dst, c, 1, n0 + i, e0 + d, P, c == 0 and (i, d) == steps[0], c == 1 and (i, d) == steps[-1])
 
         on_scalar, on_vector = nc.scalar.copy, nc.vector.tensor_copy
         gather(v2_w, tab2_w[:].bitcast(U32), idx2)
         gather(v2_s, tab2_s[:].bitcast(U8), idx2)
-        permute_wr(wr_s[:], wr_s_in[:].bitcast(U8))
+        nc.vector.tensor_copy(
+            wr_s[:].rearrange("p (c t m) -> p c t m", c=2, t=PACK),
+            wr_s_in[:].bitcast(U8).rearrange("p (c m t) -> p c t m", c=2, t=PACK),
+        )
         gather(v_w[0], tab_w[0][:].bitcast(U32), idx)
         v_s = mid.tile([P, S], U8, name="v_s", offset=4 * T, align_bytes=64)
         gather(v_s, tab_s[:].bitcast(U8), idx)
@@ -233,27 +257,47 @@ def tile_list_bipartite_edge_messages_kernel(
                 pass_ws(0, 0, g, t)
         gather(v_w[1], tab_w[1][:].bitcast(U32), idx)
         prepare_ws(1, 0, (on_vector, on_scalar))
-        for g in range(2):
-            for t in range(PACK):
-                pass_ws(1, 0, g, t)
-                tanh(0, g, t)
+        for t in range(PACK):
+            pass_ws(1, 0, 0, t)
+            tanh(0, 0, t)
+        for t in range(PACK):
+            pass_ws(1, 0, 1, t)
+            tanh(0, 1, t)
         prepare_ws(0, 1, (on_vector, on_vector))
         prepare_ws(1, 1, (on_vector, on_vector))
-        for g in range(2):
+
+        def second_block(g):
             for t in range(PACK):
                 pass_wr(1, g, t)
                 pass_ws(0, 1, g, t)
                 pass_ws(1, 1, g, t)
                 tanh(1, g, t)
-        scale_and_quantise(0, 0)
-        scale_and_quantise(1, 0)
-        scale_on_scalar(0, 1)
-        pass_wm(0, 0)
-        pass_wm(1, 0)
-        emit(0, ())
-        scale_on_scalar(1, 1)
-        scale_and_quantise(0, 1)
-        pass_wm(0, 1)
-        scale_and_quantise(1, 1)
-        pass_wm(1, 1)
-        emit(1, (1, 3))
+
+        second_block(0)
+        for t in range(PACK):
+            pass_ws(1, 1, 1, t, True)
+            pass_wr(1, 1, t, False)
+            pass_ws(0, 1, 1, t, True)
+            tanh(1, 1, t)
+        scale_on_scalar(1, 1, *TAIL[0])
+        halves = ((0, NJ // 2), (NJ // 2, NJ // 2))
+        for c in range(2):
+            scale_and_quantise(c, 0, halves)
+            for n in range(N // P):
+                pass_wm(banks[0, n][:], c, 0, n, 0, NJ, c == 0, c == 1)
+        for n in range(N // P):
+            emit(banks[0, n], n, 1, 0, NJ, False)
+        h_bf[0, 1] = keep.tile([P, PACK * NJ], BF16, name="h_bf01", tag="act10", align_bytes=64)
+        for e0, width in TAIL:
+            scale(0, 1, e0, width)
+            if e0 > 0:
+                scale(1, 1, e0, width)
+            for c in range(2):
+                quantise_h(c, 1, e0, width)
+            here = [item for item in tail_banks if item[3] == e0]
+            for c in range(2):
+                for item in here:
+                    tail_passes(c, *item)
+            for item in here:
+                bank, n0, count = item[:3]
+                emit(bank, n0, count, NJ + e0, width, item is tail_banks[-1])

@@ -23,7 +23,6 @@ KP = P * PACK
 NJ = 512
 TAB2_ROW = 8
 WR_ROW = 12
-ON_GPSIMD = 4
 RUN = 2
 TAIL = ((0, 128), (128, 256), (384, 128))
 
@@ -59,6 +58,7 @@ def tile_list_bipartite_edge_messages_kernel(
         chunks = [(c, g) for c in range(2) for g in range(2)]
         act = {k: keep.tile([P, PACK, NJ], F32, name="act%d%d" % k, tag="act%d%d" % k, align_bytes=64) for k in chunks}
         h_bf = {k: held("h_bf%d%d" % k, [P, PACK * NJ], BF16) for k in chunks if k != (0, 1)}
+        h_head = held("h_head", [P, PACK * TAIL[0][1]], BF16)
         h_w = {k: held("h_w%d%d" % k, [P, NJ], U32) for k in chunks}
         h_s = {k: held("h_s%d%d" % k, [P, NJ], U8) for k in chunks}
         banks = {(g, t): psum.tile([P, NJ], F32, name="bank%d%d" % (g, t)) for g in range(2) for t in range(PACK)}
@@ -68,25 +68,26 @@ def tile_list_bipartite_edge_messages_kernel(
             ("bm_sb", [P, N // P], F32),
         ]
         sizes = [64 * ((4 * math.prod(shape[1:]) + 63) // 64) for name, shape, dtype in later]
-        staged = late.tile([P, sum(sizes) // 4], I32, name="staged", offset=0, align_bytes=64)
-        warm = mid.tile([P, T + H // 4], F32, name="warm", offset=0, align_bytes=64)
+        staged = [
+            mid.tile([P, T + H // 4], I32, name="staged0", offset=0, align_bytes=64),
+            late.tile([P, sum(sizes) // 4], I32, name="staged1", offset=0, align_bytes=64),
+        ]
 
         def words(ap):
             return ap.rearrange("p n i -> p (n i)").bitcast(I32)
 
-        def permute_wr(dst, src):
-            dst = dst.rearrange("p (c t m) -> p c m t", c=2, t=PACK)
-            src = src.rearrange("p (c m t) -> p c m t", c=2, t=PACK)
+        def permute_wr(c):
+            dst = wr_w[:, c * KP : (c + 1) * KP].rearrange("p (t m) -> p m t", t=PACK)
+            src = staged[c][:, 0:KP].rearrange("p (m t) -> p m t", t=PACK)
             for t0 in (0, 2):
-                nc.vector.tensor_copy(dst[:, :, :, t0 : t0 + 2], src[:, :, :, t0 : t0 + 2])
+                nc.vector.tensor_copy(dst[:, :, t0 : t0 + 2], src[:, :, t0 : t0 + 2])
 
-        nc.vector.memset(warm[:, T : T + 1], 0.0)
         nc.gpsimd.memset(tab_s[:], 0)
         nc.vector.memset(tab2_s[:], 0)
-        nc.scalar.activation(warm[:, T + 1 : T + 2], warm[:, T : T + 1], ACT.Tanh)
 
+        for c in range(2):
+            nc.sync.dma_start(out=staged[c][:, 0:KP], in_=words(wr_words[0])[:, c * KP : (c + 1) * KP])
         nc.sync.dma_start(idx2[:], offs2)
-        nc.sync.dma_start(out=staged[:, 0:H], in_=words(wr_words[0]))
         nc.sync.dma_start(out=tab2_w[:], in_=words(tab2_words[0]))
         nc.sync.dma_start(idx[:], offs)
         wr_rows = wr_scales[0].rearrange("(q r) n -> r q n", r=4)
@@ -94,16 +95,16 @@ def tile_list_bipartite_edge_messages_kernel(
         for r in range(4):
             nc.sync.dma_start(out=tab2_s[TAB2_ROW + r : P : 32, :], in_=tab2_rows[r].bitcast(I32))
         for q in range(4):
-            queue = nc.gpsimd if q < ON_GPSIMD else nc.sync
-            queue.dma_start(out=tab_s[32 * q : 32 * q + 8, :], in_=tab_scales[:, 4 * q : 4 * q + 4, :].bitcast(I32))
+            nc.gpsimd.dma_start(out=tab_s[32 * q : 32 * q + 8, :], in_=tab_scales[:, 4 * q : 4 * q + 4, :].bitcast(I32))
 
+        permute_wr(0)
         tab_w0 = mid.tile([P, T], I32, name="tab_w0", offset=0, align_bytes=64)
         wr_s_in = mid.tile([P, H // 4], I32, name="wr_s_in", offset=4 * T, align_bytes=64)
         nc.vector.memset(wr_s_in[:], 0)
         nc.sync.dma_start(out=tab_w0[:], in_=words(tab_words[0]))
         for r in range(4):
             nc.sync.dma_start(out=wr_s_in[WR_ROW + r : P : 32, :], in_=wr_rows[r].bitcast(I32))
-        permute_wr(wr_w[:], staged[:, 0:H])
+        permute_wr(1)
 
         placed = {
             name: late.tile(shape, dtype, name=name, offset=sum(sizes[:i]), align_bytes=64)
@@ -174,8 +175,13 @@ def tile_list_bipartite_edge_messages_kernel(
         def tanh(c, g, t):
             nc.scalar.activation(act[c, g][:, t, :], banks[g, t][:], ACT.Tanh, bias=b_sb[:, c, t : t + 1])
 
+        def rounded(c, g, e0, width):
+            if (c, g, e0) == (0, 1, 0):
+                return h_head[:]
+            return h_bf[c, g][:, PACK * e0 : PACK * (e0 + width)]
+
         def scale(c, g, e0, width):
-            dst = h_bf[c, g][:, PACK * e0 : PACK * (e0 + width)].rearrange("p (u i t) -> p u t i", i=RUN, t=PACK)
+            dst = rounded(c, g, e0, width).rearrange("p (u i t) -> p u t i", i=RUN, t=PACK)
             src = act[c, g][:, :, e0 : e0 + width].rearrange("p t (u i) -> p u t i", i=RUN)
             factor = gain_sb[:, c, :].unsqueeze(1).unsqueeze(3).broadcast_to([P, width // RUN, PACK, RUN])
             nc.vector.tensor_tensor(dst, src, factor, ALU.mult)
@@ -186,22 +192,15 @@ def tile_list_bipartite_edge_messages_kernel(
                 nc.scalar.activation(
                     planes[:, t, :], act[c, g][:, t, e0 : e0 + width], ACT.Copy, scale=gain_sb[:, c, t : t + 1]
                 )
-            dst = h_bf[c, g][:, PACK * e0 : PACK * (e0 + width)].rearrange("p (u i t) -> p u t i", i=4, t=PACK)
+            dst = rounded(c, g, e0, width).rearrange("p (u i t) -> p u t i", i=4, t=PACK)
             nc.scalar.copy(dst, planes[:].rearrange("p t (u i) -> p u t i", i=4))
 
         def quantise_h(c, g, e0, width):
             cols = slice(e0, e0 + width)
             nc.vector.quantize_mx(
                 out=h_w[c, g][:, cols].bitcast(FP8X4), scales=h_s[c, g][:, cols],
-                in_=h_bf[c, g][:, PACK * e0 : PACK * (e0 + width)],
+                in_=rounded(c, g, e0, width),
             )
-
-        def scale_and_quantise(c, g, parts):
-            for i, part in enumerate(parts):
-                scale(c, g, *part)
-                if i > 0:
-                    quantise_h(c, g, *parts[i - 1])
-            quantise_h(c, g, *parts[-1])
 
         def pass_wm(dst, c, g, n, e0, width, start, stop):
             nc.tensor.matmul_mx(
@@ -264,6 +263,7 @@ def tile_list_bipartite_edge_messages_kernel(
             pass_ws(1, 0, 1, t)
             tanh(0, 1, t)
         prepare_ws(0, 1, (on_vector, on_vector))
+        scale(0, 0, 0, P)
         prepare_ws(1, 1, (on_vector, on_vector))
 
         def second_block(g):
@@ -282,16 +282,24 @@ def tile_list_bipartite_edge_messages_kernel(
         scale_on_scalar(1, 1, *TAIL[0])
         halves = ((0, NJ // 2), (NJ // 2, NJ // 2))
         for c in range(2):
-            scale_and_quantise(c, 0, halves)
+            if c == 0:
+                scale(0, 0, P, P)
+            else:
+                scale(1, 0, *halves[0])
+            scale(c, 0, *halves[1])
+            for part in halves:
+                quantise_h(c, 0, *part)
+            if c == 0:
+                scale(0, 1, *TAIL[0])
             for n in range(N // P):
                 pass_wm(banks[0, n][:], c, 0, n, 0, NJ, c == 0, c == 1)
         for n in range(N // P):
             emit(banks[0, n], n, 1, 0, NJ, False)
         h_bf[0, 1] = keep.tile([P, PACK * NJ], BF16, name="h_bf01", tag="act10", align_bytes=64)
         for e0, width in TAIL:
-            scale(0, 1, e0, width)
             if e0 > 0:
-                scale(1, 1, e0, width)
+                for c in range(2):
+                    scale(c, 1, e0, width)
             for c in range(2):
                 quantise_h(c, 1, e0, width)
             here = [item for item in tail_banks if item[3] == e0]

@@ -43,12 +43,13 @@ def tile_list_bipartite_edge_messages_kernel(
 
         idx = keep.tile([P, S // 16], U16, name="idx")
         idx2 = keep.tile([P, S // 16], U16, name="idx2")
-        tab_s = held("tab_s", [P, T // 4], I32)
+        v_s_spread = held("v_s_spread", [P, S], U8)
+        v_s = [held("v_s%d" % a, [P, S // 4], I32) for a in range(2)]
         tab2_w = held("tab2_w", [P, T2], I32)
         tab2_s = held("tab2_s", [P, T2 // 4], I32)
         wr_w = held("wr_w", [P, H], I32)
         wr_s = held("wr_s", [P, H], U8)
-        v_w = [held("v_w%d" % a, [P, S], U32) for a in range(2)]
+        v_w = {1: held("v_w1", [P, S], U32)}
         v2_w = held("v2_w", [P, S], U32)
         v2_s = held("v2_s", [P, S], U8)
         pieces = [(a, c, u) for a in range(2) for c in range(2) for u in range(2)]
@@ -63,15 +64,16 @@ def tile_list_bipartite_edge_messages_kernel(
         h_s = {k: held("h_s%d%d" % k, [P, NJ], U8) for k in chunks}
         banks = {(g, t): psum.tile([P, NJ], F32, name="bank%d%d" % (g, t)) for g in range(2) for t in range(PACK)}
 
-        later = [("ws_raw%d%d" % (a, c), [P, PACK, KP], F32) for c in range(2) for a in range(2)] + [
+        later = [("ws_raw%d%d" % k, [P, PACK, KP], F32) for k in ((1, 0), (0, 1), (1, 1))] + [
             ("tab_w1", [P, T], I32), ("wm_w", [P, 2, N // 2], I32), ("wm_s", [P, 2, N // 4], I32), ("gain_sb", [P, 2, PACK], F32), ("b_sb", [P, 2, PACK], F32),
             ("bm_sb", [P, N // P], F32),
         ]
         sizes = [64 * ((4 * math.prod(shape[1:]) + 63) // 64) for name, shape, dtype in later]
         staged = [
-            mid.tile([P, T + H // 4], I32, name="staged0", offset=0, align_bytes=64),
-            late.tile([P, sum(sizes) // 4], I32, name="staged1", offset=0, align_bytes=64),
+            mid.tile([P, T + S], I32, name="staged0", offset=0, align_bytes=64),
+            keep.tile([P, KP], I32, name="staged1", tag="staged1", align_bytes=64),
         ]
+        tab_s = late.tile([P, sum(sizes) // 4], I32, name="tab_s", offset=0, align_bytes=64)
 
         def words(ap):
             return ap.rearrange("p n i -> p (n i)").bitcast(I32)
@@ -82,20 +84,21 @@ def tile_list_bipartite_edge_messages_kernel(
             for t0 in (0, 2):
                 nc.vector.tensor_copy(dst[:, :, t0 : t0 + 2], src[:, :, t0 : t0 + 2])
 
-        nc.gpsimd.memset(tab_s[:], 0)
+        nc.vector.memset(tab_s[:, 0 : T // 4], 0)
         nc.vector.memset(tab2_s[:], 0)
+        for a in range(2):
+            nc.vector.memset(v_s[a][:], 0)
 
         for c in range(2):
             nc.sync.dma_start(out=staged[c][:, 0:KP], in_=words(wr_words[0])[:, c * KP : (c + 1) * KP])
         nc.sync.dma_start(idx2[:], offs2)
         nc.sync.dma_start(out=tab2_w[:], in_=words(tab2_words[0]))
         nc.sync.dma_start(idx[:], offs)
+        nc.sync.dma_start(out=tab_s[0:P:4, 0 : T // 4], in_=tab_scales.rearrange("a q n -> (a q) n").bitcast(I32))
         wr_rows = wr_scales[0].rearrange("(q r) n -> r q n", r=4)
         tab2_rows = tab2_scales[0].rearrange("(q r) n -> r q n", r=4)
         for r in range(4):
             nc.sync.dma_start(out=tab2_s[TAB2_ROW + r : P : 32, :], in_=tab2_rows[r].bitcast(I32))
-        for q in range(4):
-            nc.gpsimd.dma_start(out=tab_s[32 * q : 32 * q + 8, :], in_=tab_scales[:, 4 * q : 4 * q + 4, :].bitcast(I32))
 
         permute_wr(0)
         tab_w0 = mid.tile([P, T], I32, name="tab_w0", offset=0, align_bytes=64)
@@ -105,24 +108,38 @@ def tile_list_bipartite_edge_messages_kernel(
         for r in range(4):
             nc.sync.dma_start(out=wr_s_in[WR_ROW + r : P : 32, :], in_=wr_rows[r].bitcast(I32))
         permute_wr(1)
+        ws_rows = ws.rearrange("(a p j) r -> a p j r", a=2, j=PACK)
+        ws_first = keep.tile([P, PACK, KP], F32, name="ws_raw00", tag="staged1", align_bytes=64)
+        nc.sync.dma_start(out=ws_first[:], in_=ws_rows[0][:, :, 0:KP])
+
+        def gather(dst, window, offsets):
+            nc.vector.tensor_copy(dst[:], window.indirect(offsets[:]))
+
+        gather(v_s_spread, tab_s[:, 0 : T // 4].bitcast(U8), idx)
+
+        def carry_rows(a):
+            for r in range(4):
+                first = 64 * a + 4 * r
+                nc.sync.dma_start(out=v_s[a][4 * a + r : P : 32, :], in_=v_s_spread[first : 64 * a + 64 : 16, :].bitcast(I32))
+
+        carry_rows(0)
 
         placed = {
             name: late.tile(shape, dtype, name=name, offset=sum(sizes[:i]), align_bytes=64)
             for i, (name, shape, dtype) in enumerate(later)
         }
-        ws_raw = {(a, c): placed["ws_raw%d%d" % (a, c)][:] for a in range(2) for c in range(2)}
+        ws_raw = {k: placed["ws_raw%d%d" % k][:] for k in ((1, 0), (0, 1), (1, 1))}
+        ws_raw[0, 0] = ws_first[:]
         tab_w = [tab_w0, placed["tab_w1"]]
         wm_w, wm_s = placed["wm_w"], placed["wm_s"]
         b_sb, gain_sb, bm_sb = placed["b_sb"], placed["gain_sb"], placed["bm_sb"]
         nc.vector.memset(wm_s[:], 0)
 
-        ws_rows = ws.rearrange("(a p j) r -> a p j r", a=2, j=PACK)
-
         def load_ws(a, c):
             nc.sync.dma_start(out=ws_raw[a, c], in_=ws_rows[a][:, :, c * KP : (c + 1) * KP])
 
-        load_ws(0, 0)
         nc.sync.dma_start(out=tab_w[1][:], in_=words(tab_words[1]))
+        carry_rows(1)
         load_ws(1, 0)
         nc.sync.dma_start(out=b_sb[:], in_=b.rearrange("(c p t) -> p c t", p=P, t=PACK))
         load_ws(0, 1)
@@ -134,9 +151,6 @@ def tile_list_bipartite_edge_messages_kernel(
         wm_rows = wm_scales.rearrange("a (q r) n -> r q a n", r=4)
         for r in range(4):
             nc.sync.dma_start(out=wm_s[r:P:32, :, :], in_=wm_rows[r].bitcast(I32))
-
-        def gather(dst, window, offsets):
-            nc.vector.tensor_copy(dst[:], window.indirect(offsets[:]))
 
         def regroup_ws(engine_copy, a, c, u):
             dst = ws_bf[a, c, u][:].rearrange("p (t m j) -> p m j t", t=2, j=PACK)
@@ -168,7 +182,7 @@ def tile_list_bipartite_edge_messages_kernel(
             nc.tensor.matmul_mx(
                 out=banks[g, t][:],
                 lhsT=ws_w[a, c, t // 2][:, cols].bitcast(FP8X4), lhsT_scale=ws_s[a, c, t // 2][:, cols],
-                rhs=v_w[a][:, edges].bitcast(FP8X4), rhs_scale=v_s[4 * a : P, edges],
+                rhs=v_w[a][:, edges].bitcast(FP8X4), rhs_scale=v_s[a][:].bitcast(U8)[4 * a : P, edges],
                 start=(turned and a == 1), stop=(a == (0 if turned else 1)),
             )
 
@@ -244,9 +258,8 @@ def tile_list_bipartite_edge_messages_kernel(
             wr_s[:].rearrange("p (c t m) -> p c t m", c=2, t=PACK),
             wr_s_in[:].bitcast(U8).rearrange("p (c m t) -> p c t m", c=2, t=PACK),
         )
+        v_w[0] = mid.tile([P, S], U32, name="v_w0", offset=4 * T, align_bytes=64)
         gather(v_w[0], tab_w[0][:].bitcast(U32), idx)
-        v_s = mid.tile([P, S], U8, name="v_s", offset=4 * T, align_bytes=64)
-        gather(v_s, tab_s[:].bitcast(U8), idx)
         for g in range(2):
             for t in range(PACK):
                 pass_wr(0, g, t)

@@ -22,7 +22,7 @@ PACK = 4
 KP = P * PACK
 NJ = 512
 TAB2_ROW = 8
-WR_ROW = 12
+WR_ROWS = (8, 12)
 RUN = 2
 TAIL = ((0, 128), (128, 256), (384, 128))
 
@@ -48,7 +48,7 @@ def tile_list_bipartite_edge_messages_kernel(
         tab2_w = held("tab2_w", [P, T2], I32)
         tab2_s = held("tab2_s", [P, T2 // 4], I32)
         wr_w = held("wr_w", [P, H], I32)
-        wr_s = held("wr_s", [P, H], U8)
+        wr_s = held("wr_s", [P, KP], U8)
         v_w = {1: held("v_w1", [P, S], U32)}
         v2_w = held("v2_w", [P, S], U32)
         v2_s = held("v2_s", [P, S], U8)
@@ -64,8 +64,8 @@ def tile_list_bipartite_edge_messages_kernel(
         h_s = {k: held("h_s%d%d" % k, [P, NJ], U8) for k in chunks}
         banks = {(g, t): psum.tile([P, NJ], F32, name="bank%d%d" % (g, t)) for g in range(2) for t in range(PACK)}
 
-        later = [("ws_raw%d%d" % k, [P, PACK, KP], F32) for k in ((1, 0), (0, 1), (1, 1))] + [
-            ("tab_w1", [P, T], I32), ("wm_w", [P, 2, N // 2], I32), ("wm_s", [P, 2, N // 4], I32), ("gain_sb", [P, 2, PACK], F32), ("b_sb", [P, 2, PACK], F32),
+        later = [("ws_raw%d%d" % k, [P, PACK, KP], F32) for k in ((1, 0), (0, 1))] + [("ws_last%d" % half, [P, PACK, KP // 2], F32) for half in range(2)] + [
+            ("tab_w1", [P, T], I32), ("wm_w", [P, 2, N // 2], I32), ("wm_s", [P, 2, N // 4], I32), ("gain_sb", [P, 2, PACK], F32), ("b_sb0", [P, PACK], F32), ("b_sb1", [P, PACK], F32),
             ("bm_sb", [P, N // P], F32),
         ]
         sizes = [64 * ((4 * math.prod(shape[1:]) + 63) // 64) for name, shape, dtype in later]
@@ -94,19 +94,19 @@ def tile_list_bipartite_edge_messages_kernel(
         nc.sync.dma_start(idx2[:], offs2)
         nc.sync.dma_start(out=tab2_w[:], in_=words(tab2_words[0]))
         nc.sync.dma_start(idx[:], offs)
-        nc.sync.dma_start(out=tab_s[0:P:4, 0 : T // 4], in_=tab_scales.rearrange("a q n -> (a q) n").bitcast(I32))
-        wr_rows = wr_scales[0].rearrange("(q r) n -> r q n", r=4)
+        nc.scalar.dma_start(out=tab_s[0:P:4, 0 : T // 4], in_=tab_scales.rearrange("a q n -> (a q) n").bitcast(I32))
+        wr_rows = wr_scales[0].rearrange("(q r) (c n) -> q c r n", r=4, c=2)
         tab2_rows = tab2_scales[0].rearrange("(q r) n -> r q n", r=4)
         for r in range(4):
             nc.sync.dma_start(out=tab2_s[TAB2_ROW + r : P : 32, :], in_=tab2_rows[r].bitcast(I32))
 
         permute_wr(0)
         tab_w0 = mid.tile([P, T], I32, name="tab_w0", offset=0, align_bytes=64)
-        wr_s_in = mid.tile([P, H // 4], I32, name="wr_s_in", offset=4 * T, align_bytes=64)
+        wr_s_in = mid.tile([P, KP // 4], I32, name="wr_s_in", offset=4 * T, align_bytes=64)
         nc.vector.memset(wr_s_in[:], 0)
         nc.sync.dma_start(out=tab_w0[:], in_=words(tab_words[0]))
-        for r in range(4):
-            nc.sync.dma_start(out=wr_s_in[WR_ROW + r : P : 32, :], in_=wr_rows[r].bitcast(I32))
+        for q in range(4):
+            nc.sync.dma_start(out=wr_s_in[32 * q + 8 : 32 * q + 16, :], in_=wr_rows[q].bitcast(I32))
         permute_wr(1)
         ws_rows = ws.rearrange("(a p j) r -> a p j r", a=2, j=PACK)
         ws_first = keep.tile([P, PACK, KP], F32, name="ws_raw00", tag="staged1", align_bytes=64)
@@ -128,11 +128,12 @@ def tile_list_bipartite_edge_messages_kernel(
             name: late.tile(shape, dtype, name=name, offset=sum(sizes[:i]), align_bytes=64)
             for i, (name, shape, dtype) in enumerate(later)
         }
-        ws_raw = {k: placed["ws_raw%d%d" % k][:] for k in ((1, 0), (0, 1), (1, 1))}
+        ws_raw = {k: placed["ws_raw%d%d" % k][:] for k in ((1, 0), (0, 1))}
+        ws_last = [placed["ws_last%d" % half] for half in range(2)]
         ws_raw[0, 0] = ws_first[:]
         tab_w = [tab_w0, placed["tab_w1"]]
         wm_w, wm_s = placed["wm_w"], placed["wm_s"]
-        b_sb, gain_sb, bm_sb = placed["b_sb"], placed["gain_sb"], placed["bm_sb"]
+        b_sb, gain_sb, bm_sb = [placed["b_sb0"], placed["b_sb1"]], placed["gain_sb"], placed["bm_sb"]
         nc.vector.memset(wm_s[:], 0)
 
         def load_ws(a, c):
@@ -141,9 +142,12 @@ def tile_list_bipartite_edge_messages_kernel(
         nc.sync.dma_start(out=tab_w[1][:], in_=words(tab_words[1]))
         carry_rows(1)
         load_ws(1, 0)
-        nc.sync.dma_start(out=b_sb[:], in_=b.rearrange("(c p t) -> p c t", p=P, t=PACK))
+        b_rows = b.rearrange("(c p t) -> c p t", p=P, t=PACK)
+        nc.sync.dma_start(out=b_sb[0][:], in_=b_rows[0])
         load_ws(0, 1)
-        load_ws(1, 1)
+        for half in range(2):
+            nc.sync.dma_start(out=ws_last[half][:], in_=ws_rows[1][:, :, KP + half * KP // 2 : KP + (half + 1) * KP // 2])
+        nc.sync.dma_start(out=b_sb[1][:], in_=b_rows[1])
         nc.sync.dma_start(out=gain_sb[:], in_=gain.rearrange("(c p t) -> p c t", p=P, t=PACK))
         nc.sync.dma_start(out=wm_w[:], in_=wm_words.rearrange("a p n -> p a n").bitcast(I32))
         with nc.allow_non_contiguous_dma(reason="one bias value a partition"):
@@ -171,7 +175,7 @@ def tile_list_bipartite_edge_messages_kernel(
             edges = slice(g * NJ, (g + 1) * NJ)
             nc.tensor.matmul_mx(
                 out=banks[g, t][:],
-                lhsT=wr_w[:, cols].bitcast(FP8X4), lhsT_scale=wr_s[WR_ROW:P, cols],
+                lhsT=wr_w[:, cols].bitcast(FP8X4), lhsT_scale=wr_s[WR_ROWS[c] : P, t * P : (t + 1) * P],
                 rhs=v2_w[:, edges].bitcast(FP8X4), rhs_scale=v2_s[TAB2_ROW:P, edges],
                 start=start, stop=False,
             )
@@ -187,7 +191,7 @@ def tile_list_bipartite_edge_messages_kernel(
             )
 
         def tanh(c, g, t):
-            nc.scalar.activation(act[c, g][:, t, :], banks[g, t][:], ACT.Tanh, bias=b_sb[:, c, t : t + 1])
+            nc.scalar.activation(act[c, g][:, t, :], banks[g, t][:], ACT.Tanh, bias=b_sb[c][:, t : t + 1])
 
         def rounded(c, g, e0, width):
             if (c, g, e0) == (0, 1, 0):
@@ -255,8 +259,8 @@ def tile_list_bipartite_edge_messages_kernel(
         gather(v2_w, tab2_w[:].bitcast(U32), idx2)
         gather(v2_s, tab2_s[:].bitcast(U8), idx2)
         nc.vector.tensor_copy(
-            wr_s[:].rearrange("p (c t m) -> p c t m", c=2, t=PACK),
-            wr_s_in[:].bitcast(U8).rearrange("p (c m t) -> p c t m", c=2, t=PACK),
+            wr_s[:].rearrange("p (t m) -> p t m", t=PACK),
+            wr_s_in[:].bitcast(U8).rearrange("p (m t) -> p t m", t=PACK),
         )
         v_w[0] = mid.tile([P, S], U32, name="v_w0", offset=4 * T, align_bytes=64)
         gather(v_w[0], tab_w[0][:].bitcast(U32), idx)
@@ -277,7 +281,13 @@ def tile_list_bipartite_edge_messages_kernel(
             tanh(0, 1, t)
         prepare_ws(0, 1, (on_vector, on_vector))
         scale(0, 0, 0, P)
-        prepare_ws(1, 1, (on_vector, on_vector))
+        for half in range(2):
+            for u in range(2):
+                dst = ws_bf[1, 1, u][:].rearrange("p (t m j) -> p m j t", t=2, j=PACK)[:, half * P // 2 : (half + 1) * P // 2]
+                src = ws_last[half][:].rearrange("p j (m t) -> p m j t", t=PACK)
+                on_vector(dst, src[:, :, :, 2 * u : 2 * u + 2])
+        for u in range(2):
+            quantise_ws(1, 1, u)
 
         def second_block(g):
             for t in range(PACK):

@@ -1,4 +1,3 @@
-import math
 from contextlib import ExitStack
 
 import concourse.mybir as mybir
@@ -21,10 +20,11 @@ P = 128
 PACK = 4
 KP = P * PACK
 NJ = 512
+NQ = 256
 TAB2_ROW = 8
 WR_ROWS = (8, 12)
 RUN = 2
-TAIL = ((0, 128), (128, 256), (384, 128))
+KIB = 1024
 
 
 def tile_list_bipartite_edge_messages_kernel(
@@ -34,120 +34,239 @@ def tile_list_bipartite_edge_messages_kernel(
     nc = tc.nc
     with ExitStack() as ctx:
         keep = ctx.enter_context(tc.tile_pool(name="keep", bufs=1))
-        mid = ctx.enter_context(tc.tile_pool(name="mid", bufs=1))
-        late = ctx.enter_context(tc.tile_pool(name="late", bufs=1))
+        rooms = [ctx.enter_context(tc.tile_pool(name="room%d" % i, bufs=1)) for i in range(5)]
         psum = ctx.enter_context(tc.psum_pool(name="psum", bufs=1))
 
-        def held(name, shape, dtype):
-            return keep.tile(shape, dtype, name=name, align_bytes=64)
+        def held(name, shape, dtype, tag=None):
+            return keep.tile(shape, dtype, name=name, tag=tag or name, align_bytes=64)
 
-        idx = keep.tile([P, S // 16], U16, name="idx")
-        idx2 = keep.tile([P, S // 16], U16, name="idx2")
-        v_s_spread = held("v_s_spread", [P, S], U8)
-        v_s = [held("v_s%d" % a, [P, S // 4], I32) for a in range(2)]
-        tab2_w = held("tab2_w", [P, T2], I32)
-        tab2_s = held("tab2_s", [P, T2 // 4], I32)
-        wr_w = held("wr_w", [P, H], I32)
-        wr_s = held("wr_s", [P, KP], U8)
-        v_w = {1: held("v_w1", [P, S], U32)}
-        v2_w = held("v2_w", [P, S], U32)
-        v2_s = held("v2_s", [P, S], U8)
-        pieces = [(a, c, u) for a in range(2) for c in range(2) for u in range(2)]
-        ws_bf = {k: held("ws_bf%d%d%d" % k, [P, 2 * KP], BF16) for k in pieces}
-        ws_w = {k: held("ws_w%d%d%d" % k, [P, 2 * P], U32) for k in pieces}
-        ws_s = {k: held("ws_s%d%d%d" % k, [P, 2 * P], U8) for k in pieces}
-        chunks = [(c, g) for c in range(2) for g in range(2)]
-        act = {k: keep.tile([P, PACK, NJ], F32, name="act%d%d" % k, tag="act%d%d" % k, align_bytes=64) for k in chunks}
-        h_bf = {k: held("h_bf%d%d" % k, [P, PACK * NJ], BF16) for k in chunks if k != (0, 1)}
-        h_head = held("h_head", [P, PACK * TAIL[0][1]], BF16)
-        h_w = {k: held("h_w%d%d" % k, [P, NJ], U32) for k in chunks}
-        h_s = {k: held("h_s%d%d" % k, [P, NJ], U8) for k in chunks}
-        banks = {(g, t): psum.tile([P, NJ], F32, name="bank%d%d" % (g, t)) for g in range(2) for t in range(PACK)}
-
-        later = [("ws_raw%d%d" % k, [P, PACK, KP], F32) for k in ((1, 0), (0, 1))] + [("ws_last%d" % half, [P, PACK, KP // 2], F32) for half in range(2)] + [
-            ("tab_w1", [P, T], I32), ("wm_w", [P, 2, N // 2], I32), ("wm_s", [P, 2, N // 4], I32), ("gain_sb", [P, 2, PACK], F32), ("b_sb0", [P, PACK], F32), ("b_sb1", [P, PACK], F32),
-            ("bm_sb", [P, N // P], F32),
-        ]
-        sizes = [64 * ((4 * math.prod(shape[1:]) + 63) // 64) for name, shape, dtype in later]
-        staged = [
-            mid.tile([P, T + S], I32, name="staged0", offset=0, align_bytes=64),
-            keep.tile([P, KP], I32, name="staged1", tag="staged1", align_bytes=64),
-        ]
-        tab_s = late.tile([P, sum(sizes) // 4], I32, name="tab_s", offset=0, align_bytes=64)
+        def placed(room, offset, name, shape, dtype):
+            return rooms[room].tile(shape, dtype, name=name, offset=offset, align_bytes=64)
 
         def words(ap):
             return ap.rearrange("p n i -> p (n i)").bitcast(I32)
 
-        def permute_wr(c):
-            dst = wr_w[:, c * KP : (c + 1) * KP].rearrange("p (t m) -> p m t", t=PACK)
-            src = staged[c][:, 0:KP].rearrange("p (m t) -> p m t", t=PACK)
-            for t0 in (0, 2):
-                nc.vector.tensor_copy(dst[:, :, t0 : t0 + 2], src[:, :, t0 : t0 + 2])
+        idx = keep.tile([P, S // 16], U16, name="idx")
+        idx2 = keep.tile([P, S // 16], U16, name="idx2")
+        banks = [psum.tile([P, NJ], F32, name="bank%d" % i) for i in range(8)]
+        wr_in = [placed(0, 15 * KIB, "wr_in0", [P, KP], I32), placed(4, 2 * KIB - 64, "wr_in1", [P, KP], I32)]
+        tab_s = placed(1, 8 * KIB - 64, "tab_s", [P, T // 4], I32)
+        tab2_w = placed(2, 0, "tab2_w", [P, T2], I32)
+        tab2_s = placed(3, 0, "tab2_s", [P, T2 // 4], I32)
+        wr_w = held("wr_w", [P, H], I32)
+        wr_s = held("wr_s", [P, KP], U8)
+        v_s = [held("v_s%d" % a, [P, S // 4], I32) for a in range(2)]
+        pieces = [(a, c, u) for a in range(2) for c in range(2) for u in range(2)]
+        ws_bf = {k: held("ws_bf%d%d%d" % k, [P, 2 * KP], BF16) for k in pieces}
+        ws_w = {k: held("ws_w%d%d%d" % k, [P, 2 * P], U32) for k in pieces}
+        ws_s = {k: held("ws_s%d%d%d" % k, [P, 2 * P], U8) for k in pieces}
 
-        nc.vector.memset(tab_s[:, 0 : T // 4], 0)
-        nc.vector.memset(tab2_s[:], 0)
-        for a in range(2):
-            nc.vector.memset(v_s[a][:], 0)
+        for tile in (tab_s, tab2_s, v_s[0], v_s[1]):
+            nc.vector.memset(tile[:], 0)
 
         for c in range(2):
-            nc.sync.dma_start(out=staged[c][:, 0:KP], in_=words(wr_words[0])[:, c * KP : (c + 1) * KP])
+            nc.sync.dma_start(out=wr_in[c][:], in_=words(wr_words[0])[:, c * KP : (c + 1) * KP])
         nc.sync.dma_start(idx2[:], offs2)
-        nc.sync.dma_start(out=tab2_w[:], in_=words(tab2_words[0]))
         nc.sync.dma_start(idx[:], offs)
-        nc.scalar.dma_start(out=tab_s[0:P:4, 0 : T // 4], in_=tab_scales.rearrange("a q n -> (a q) n").bitcast(I32))
-        wr_rows = wr_scales[0].rearrange("(q r) (c n) -> q c r n", r=4, c=2)
+        nc.sync.dma_start(out=tab_s[0:P:4, :], in_=tab_scales.rearrange("a q n -> (a q) n").bitcast(I32))
+        nc.sync.dma_start(out=tab2_w[:], in_=words(tab2_words[0]))
         tab2_rows = tab2_scales[0].rearrange("(q r) n -> r q n", r=4)
         for r in range(4):
             nc.sync.dma_start(out=tab2_s[TAB2_ROW + r : P : 32, :], in_=tab2_rows[r].bitcast(I32))
 
+
+        def permute_wr(c):
+            dst = wr_w[:, c * KP : (c + 1) * KP].rearrange("p (t m) -> p m t", t=PACK)
+            src = wr_in[c][:].rearrange("p (m t) -> p m t", t=PACK)
+            for t0 in (0, 2):
+                nc.vector.tensor_copy(dst[:, :, t0 : t0 + 2], src[:, :, t0 : t0 + 2])
+
+        ws_rows = ws.rearrange("(a p j) r -> a p j r", a=2, j=PACK)
+
+        def load_ws(tile, a, c0, width):
+            nc.sync.dma_start(out=tile[:], in_=ws_rows[a][:, :, c0 : c0 + width])
+
+        def gather(dst, window, offsets):
+            nc.vector.tensor_copy(dst, window.indirect(offsets))
+
+        def carry(a):
+            for r in range(4):
+                src = spread[64 * a + 4 * r : 64 * a + 64 : 16, :]
+                nc.sync.dma_start(out=v_s[a][4 * a + r : P : 32, :], in_=src.bitcast(I32))
+
         permute_wr(0)
-        tab_w0 = mid.tile([P, T], I32, name="tab_w0", offset=0, align_bytes=64)
-        wr_s_in = mid.tile([P, KP // 4], I32, name="wr_s_in", offset=4 * T, align_bytes=64)
+        tab_w = [placed(0, 0, "tab_w0", [P, T], I32)]
+        wr_s_in = placed(0, 16 * KIB, "wr_s_in", [P, KP // 4], I32)
         nc.vector.memset(wr_s_in[:], 0)
-        nc.sync.dma_start(out=tab_w0[:], in_=words(tab_words[0]))
+        nc.sync.dma_start(out=tab_w[0][:], in_=words(tab_words[0]))
+        wr_rows = wr_scales[0].rearrange("(q r) (c n) -> q c r n", r=4, c=2)
         for q in range(4):
             nc.sync.dma_start(out=wr_s_in[32 * q + 8 : 32 * q + 16, :], in_=wr_rows[q].bitcast(I32))
         permute_wr(1)
-        ws_rows = ws.rearrange("(a p j) r -> a p j r", a=2, j=PACK)
-        ws_first = keep.tile([P, PACK, KP], F32, name="ws_raw00", tag="staged1", align_bytes=64)
-        nc.sync.dma_start(out=ws_first[:], in_=ws_rows[0][:, :, 0:KP])
+        ws_raw = {(0, 0): placed(4, 3 * KIB, "ws_raw00", [P, PACK, KP], F32)}
+        load_ws(ws_raw[0, 0], 0, 0, KP)
 
-        def gather(dst, window, offsets):
-            nc.vector.tensor_copy(dst[:], window.indirect(offsets[:]))
-
-        gather(v_s_spread, tab_s[:, 0 : T // 4].bitcast(U8), idx)
-
-        def carry_rows(a):
-            for r in range(4):
-                first = 64 * a + 4 * r
-                nc.sync.dma_start(out=v_s[a][4 * a + r : P : 32, :], in_=v_s_spread[first : 64 * a + 64 : 16, :].bitcast(I32))
-
-        carry_rows(0)
-
-        placed = {
-            name: late.tile(shape, dtype, name=name, offset=sum(sizes[:i]), align_bytes=64)
-            for i, (name, shape, dtype) in enumerate(later)
-        }
-        ws_raw = {k: placed["ws_raw%d%d" % k][:] for k in ((1, 0), (0, 1))}
-        ws_last = [placed["ws_last%d" % half] for half in range(2)]
-        ws_raw[0, 0] = ws_first[:]
-        tab_w = [tab_w0, placed["tab_w1"]]
-        wm_w, wm_s = placed["wm_w"], placed["wm_s"]
-        b_sb, gain_sb, bm_sb = [placed["b_sb0"], placed["b_sb1"]], placed["gain_sb"], placed["bm_sb"]
-        nc.vector.memset(wm_s[:], 0)
-
-        def load_ws(a, c):
-            nc.sync.dma_start(out=ws_raw[a, c], in_=ws_rows[a][:, :, c * KP : (c + 1) * KP])
-
+        spread = placed(4, 2 * KIB, "spread", [P, S], U8)
+        gather(spread[:], tab_s[:].bitcast(U8), idx[:])
+        ws_raw[1, 0] = placed(1, 0, "ws_raw10", [P, PACK, KP], F32)
+        b_sb = placed(1, 8 * KIB, "b_sb", [P, 2, PACK], F32)
+        tab_w.append(placed(1, 11 * KIB + 64, "tab_w1", [P, T], I32))
+        load_ws(ws_raw[1, 0], 1, 0, KP)
+        carry(0)
         nc.sync.dma_start(out=tab_w[1][:], in_=words(tab_words[1]))
-        carry_rows(1)
-        load_ws(1, 0)
-        b_rows = b.rearrange("(c p t) -> c p t", p=P, t=PACK)
-        nc.sync.dma_start(out=b_sb[0][:], in_=b_rows[0])
-        load_ws(0, 1)
+        carry(1)
+        nc.sync.dma_start(out=b_sb[:], in_=b.rearrange("(c p t) -> p c t", p=P, t=PACK))
+
+        v2_w = [placed(1, 8 * KIB + 64, "v2_w0", [P, NJ], U32)]
+        v2_s = placed(1, 10 * KIB + 64, "v2_s", [P, S], U8)
+        gather(v2_w[0][:], tab2_w[:].bitcast(U32), idx2[:, 0 : NJ // 16])
+        gather(v2_s[:], tab2_s[:].bitcast(U8), idx2[:])
+        v2_w.append(placed(3, 0, "v2_w1", [P, NJ], U32))
+        gather(v2_w[1][:], tab2_w[:].bitcast(U32), idx2[:, NJ // 16 :])
+        ws_raw[0, 1] = placed(2, 0, "ws_raw01", [P, PACK, KP], F32)
+        load_ws(ws_raw[0, 1], 0, KP, KP)
+        nc.vector.tensor_copy(
+            wr_s[:].rearrange("p (t m) -> p t m", t=PACK),
+            wr_s_in[:].bitcast(U8).rearrange("p (m t) -> p t m", t=PACK),
+        )
+
+        v_w = {}
+
+        def gather_words(a, e0, width):
+            v_w[a, e0] = held("v_w%d_%d" % (a, e0), [P, width], U32)
+            gather(v_w[a, e0][:], tab_w[a][:].bitcast(U32), idx[:, e0 // 16 : (e0 + width) // 16])
+
+        def looked_up(a, e0, width):
+            first = max(k[1] for k in v_w if k[0] == a and k[1] <= e0)
+            return v_w[a, first][:, e0 - first : e0 - first + width]
+
+        v_w[0, 0] = placed(0, 16 * KIB, "v_w0", [P, NJ], U32)
+        gather(v_w[0, 0][:], tab_w[0][:].bitcast(U32), idx[:, 0 : NJ // 16])
+        def regroup(copy, raw, a, c, u, m0=0, count=P):
+            dst = ws_bf[a, c, u][:].rearrange("p (t m j) -> p m j t", t=2, j=PACK)[:, m0 : m0 + count]
+            src = raw[:].rearrange("p j (m t) -> p m j t", t=PACK)
+            copy(dst, src[:, :, :, 2 * u : 2 * u + 2])
+
+        def quantise_ws(a, c, u):
+            nc.vector.quantize_mx(out=ws_w[a, c, u][:].bitcast(FP8X4), scales=ws_s[a, c, u][:], in_=ws_bf[a, c, u][:])
+
+        def prepare_ws(copy, a, c):
+            for u in range(2):
+                regroup(copy, ws_raw[a, c], a, c, u)
+            for u in range(2):
+                quantise_ws(a, c, u)
+
+        def pass_wr(bank, c, g, t, start=True):
+            cols = slice(c * KP + t * P, c * KP + (t + 1) * P)
+            nc.tensor.matmul_mx(
+                out=banks[bank][:],
+                lhsT=wr_w[:, cols].bitcast(FP8X4), lhsT_scale=wr_s[WR_ROWS[c] : P, t * P : (t + 1) * P],
+                rhs=v2_w[g][:].bitcast(FP8X4),
+                rhs_scale=v2_s[TAB2_ROW:P, g * NJ : (g + 1) * NJ],
+                start=start, stop=False,
+            )
+
+        def pass_ws(bank, a, c, g, t, start=False, stop=False):
+            cols = slice(t % 2 * P, (t % 2 + 1) * P)
+            nc.tensor.matmul_mx(
+                out=banks[bank][:],
+                lhsT=ws_w[a, c, t // 2][:, cols].bitcast(FP8X4), lhsT_scale=ws_s[a, c, t // 2][:, cols],
+                rhs=looked_up(a, g * NJ, NJ).bitcast(FP8X4),
+                rhs_scale=v_s[a][:].bitcast(U8)[4 * a : P, g * NJ : (g + 1) * NJ],
+                start=start, stop=stop,
+            )
+
+        act = {(c, g): held("act%d%d" % (c, g), [P, PACK, NJ], F32) for c in range(2) for g in range(2)}
+        h_w = {k: held("h_w%d%d" % k, [P, NJ], U32) for k in act}
+        h_s = {k: held("h_s%d%d" % k, [P, NJ], U8) for k in act}
+
+        def tanh(bank, c, g, t):
+            nc.scalar.activation(act[c, g][:, t, :], banks[bank][:], ACT.Tanh, bias=b_sb[:, c, t : t + 1])
+
+        def whole_sum(bank, c, g, t):
+            pass_wr(bank, c, g, t)
+            pass_ws(bank, 0, c, g, t)
+            pass_ws(bank, 1, c, g, t, stop=True)
+            tanh(bank, c, g, t)
+
+        h_bf = {}
+
+        def scale(c, e0, width, tag=None):
+            g, first = divmod(e0, NJ)
+            h_bf[c, e0] = held("h_bf%d_%d" % (c, e0), [P, PACK * width], BF16, tag)
+            dst = h_bf[c, e0][:].rearrange("p (u i t) -> p u t i", i=RUN, t=PACK)
+            src = act[c, g][:, :, first : first + width].rearrange("p t (u i) -> p u t i", i=RUN)
+            factor = gain_sb[:, c, :].unsqueeze(1).unsqueeze(3).broadcast_to([P, width // RUN, PACK, RUN])
+            nc.vector.tensor_tensor(dst, src, factor, ALU.mult)
+
+        def scale_on_scalar(c, e0, width):
+            g, first = divmod(e0, NJ)
+            planes = held("planes", [P, PACK, width], BF16)
+            for t in range(PACK):
+                nc.scalar.activation(
+                    planes[:, t, :], act[c, g][:, t, first : first + width], ACT.Copy, scale=gain_sb[:, c, t : t + 1]
+                )
+            h_bf[c, e0] = held("h_bf%d_%d" % (c, e0), [P, PACK * width], BF16)
+            dst = h_bf[c, e0][:].rearrange("p (u i t) -> p u t i", i=4, t=PACK)
+            nc.scalar.copy(dst, planes[:].rearrange("p t (u i) -> p u t i", i=4))
+
+        def quantise_h(c, e0, width):
+            g, first = divmod(e0, NJ)
+            cols = slice(first, first + width)
+            nc.vector.quantize_mx(out=h_w[c, g][:, cols].bitcast(FP8X4), scales=h_s[c, g][:, cols], in_=h_bf[c, e0][:])
+
+        def second_product(c, e0, width, where):
+            g, first = divmod(e0, NJ)
+            count = N // P // len(where)
+            for n in range(N // P):
+                i = n % count
+                nc.tensor.matmul_mx(
+                    out=banks[where[n // count]][:, i * width : (i + 1) * width],
+                    lhsT=wm_w[:, c, :].bitcast(U8)[:, 2 * n * P : 2 * (n + 1) * P].bitcast(FP4X4),
+                    lhsT_scale=wm_s[:, c, :].bitcast(U8)[:, n * P : (n + 1) * P],
+                    rhs=h_w[c, g][:, first : first + width].bitcast(FP8X4), rhs_scale=h_s[c, g][:, first : first + width],
+                    start=(c == 0 and i == 0), stop=(c == 1 and i == count - 1),
+                )
+
+        out_rows = out.rearrange("(n p) e -> p n e", p=P)
+
+        def emit(bank, n0, count, e0, width, on_vector=False):
+            res = keep.tile([P, count, width], F32, name="res%d_%d" % (n0, e0))
+            done = banks[bank][:, 0 : count * width].rearrange("p (n e) -> p n e", n=count)
+            if on_vector:
+                shift = bm_sb[:, n0 : n0 + count].unsqueeze(2).broadcast_to([P, count, width])
+                nc.vector.tensor_tensor(res[:], done, shift, ALU.add)
+            else:
+                for i in range(count):
+                    nc.scalar.activation(res[:, i, :], done[:, i, :], ACT.Identity, bias=bm_sb[:, n0 + i : n0 + i + 1])
+            nc.sync.dma_start(out=out_rows[:, n0 : n0 + count, e0 : e0 + width], in_=res[:])
+
+        def messages(e0, width, where, last=False):
+            for c in range(2):
+                second_product(c, e0, width, where)
+            count = N // P // len(where)
+            for k, bank in enumerate(where):
+                emit(bank, k * count, count, e0, width, last and k == 1)
+
+        ahead = [(bank, bank // PACK, bank % PACK) for bank in range(8)]
+        for bank, g, t in ahead:
+            pass_wr(bank, 0, g, t)
+        prepare_ws(nc.scalar.copy, 0, 0)
+        for t in range(PACK):
+            pass_ws(t, 0, 0, 0, t)
+        prepare_ws(nc.scalar.copy, 1, 0)
+        v_w[0, NJ] = held("v_w0_last", [P, NJ], U32, "ws_bf100")
+        gather(v_w[0, NJ][:], tab_w[0][:].bitcast(U32), idx[:, NJ // 16 :])
+        for bank, g, t in ahead[PACK:]:
+            pass_ws(bank, 0, 0, g, t)
+        ws_last = [placed(0, 4 * KIB * half, "ws_last%d" % half, [P, PACK, KP // 2], F32) for half in range(2)]
+        wm_w = placed(0, 8 * KIB, "wm_w", [P, 2, N // 2], I32)
+        wm_s = placed(0, 10 * KIB, "wm_s", [P, 2, N // 4], I32)
+        bm_sb = placed(0, 11 * KIB, "bm_sb", [P, N // P], F32)
+        gain_sb = placed(0, 12 * KIB, "gain_sb", [P, 2, PACK], F32)
+        nc.vector.memset(wm_s[:], 0)
         for half in range(2):
-            nc.sync.dma_start(out=ws_last[half][:], in_=ws_rows[1][:, :, KP + half * KP // 2 : KP + (half + 1) * KP // 2])
-        nc.sync.dma_start(out=b_sb[1][:], in_=b_rows[1])
+            load_ws(ws_last[half], 1, KP + half * KP // 2, KP // 2)
         nc.sync.dma_start(out=gain_sb[:], in_=gain.rearrange("(c p t) -> p c t", p=P, t=PACK))
         nc.sync.dma_start(out=wm_w[:], in_=wm_words.rearrange("a p n -> p a n").bitcast(I32))
         with nc.allow_non_contiguous_dma(reason="one bias value a partition"):
@@ -156,179 +275,39 @@ def tile_list_bipartite_edge_messages_kernel(
         for r in range(4):
             nc.sync.dma_start(out=wm_s[r:P:32, :, :], in_=wm_rows[r].bitcast(I32))
 
-        def regroup_ws(engine_copy, a, c, u):
-            dst = ws_bf[a, c, u][:].rearrange("p (t m j) -> p m j t", t=2, j=PACK)
-            src = ws_raw[a, c].rearrange("p j (m t) -> p m j t", t=PACK)
-            engine_copy(dst, src[:, :, :, 2 * u : 2 * u + 2])
-
-        def quantise_ws(a, c, u):
-            nc.vector.quantize_mx(out=ws_w[a, c, u][:].bitcast(FP8X4), scales=ws_s[a, c, u][:], in_=ws_bf[a, c, u][:])
-
-        def prepare_ws(a, c, copies):
-            for u in range(2):
-                regroup_ws(copies[u], a, c, u)
-            for u in range(2):
-                quantise_ws(a, c, u)
-
-        def pass_wr(c, g, t, start=True):
-            cols = slice(c * KP + t * P, c * KP + (t + 1) * P)
-            edges = slice(g * NJ, (g + 1) * NJ)
-            nc.tensor.matmul_mx(
-                out=banks[g, t][:],
-                lhsT=wr_w[:, cols].bitcast(FP8X4), lhsT_scale=wr_s[WR_ROWS[c] : P, t * P : (t + 1) * P],
-                rhs=v2_w[:, edges].bitcast(FP8X4), rhs_scale=v2_s[TAB2_ROW:P, edges],
-                start=start, stop=False,
-            )
-
-        def pass_ws(a, c, g, t, turned=False):
-            cols = slice(t % 2 * P, (t % 2 + 1) * P)
-            edges = slice(g * NJ, (g + 1) * NJ)
-            nc.tensor.matmul_mx(
-                out=banks[g, t][:],
-                lhsT=ws_w[a, c, t // 2][:, cols].bitcast(FP8X4), lhsT_scale=ws_s[a, c, t // 2][:, cols],
-                rhs=v_w[a][:, edges].bitcast(FP8X4), rhs_scale=v_s[a][:].bitcast(U8)[4 * a : P, edges],
-                start=(turned and a == 1), stop=(a == (0 if turned else 1)),
-            )
-
-        def tanh(c, g, t):
-            nc.scalar.activation(act[c, g][:, t, :], banks[g, t][:], ACT.Tanh, bias=b_sb[c][:, t : t + 1])
-
-        def rounded(c, g, e0, width):
-            if (c, g, e0) == (0, 1, 0):
-                return h_head[:]
-            return h_bf[c, g][:, PACK * e0 : PACK * (e0 + width)]
-
-        def scale(c, g, e0, width):
-            dst = rounded(c, g, e0, width).rearrange("p (u i t) -> p u t i", i=RUN, t=PACK)
-            src = act[c, g][:, :, e0 : e0 + width].rearrange("p t (u i) -> p u t i", i=RUN)
-            factor = gain_sb[:, c, :].unsqueeze(1).unsqueeze(3).broadcast_to([P, width // RUN, PACK, RUN])
-            nc.vector.tensor_tensor(dst, src, factor, ALU.mult)
-
-        def scale_on_scalar(c, g, e0, width):
-            planes = held("planes", [P, PACK, width], BF16)
-            for t in range(PACK):
-                nc.scalar.activation(
-                    planes[:, t, :], act[c, g][:, t, e0 : e0 + width], ACT.Copy, scale=gain_sb[:, c, t : t + 1]
-                )
-            dst = rounded(c, g, e0, width).rearrange("p (u i t) -> p u t i", i=4, t=PACK)
-            nc.scalar.copy(dst, planes[:].rearrange("p t (u i) -> p u t i", i=4))
-
-        def quantise_h(c, g, e0, width):
-            cols = slice(e0, e0 + width)
-            nc.vector.quantize_mx(
-                out=h_w[c, g][:, cols].bitcast(FP8X4), scales=h_s[c, g][:, cols],
-                in_=rounded(c, g, e0, width),
-            )
-
-        def pass_wm(dst, c, g, n, e0, width, start, stop):
-            nc.tensor.matmul_mx(
-                out=dst,
-                lhsT=wm_w[:, c, :].bitcast(U8)[:, 2 * n * P : 2 * (n + 1) * P].bitcast(FP4X4),
-                lhsT_scale=wm_s[:, c, :].bitcast(U8)[:, n * P : (n + 1) * P],
-                rhs=h_w[c, g][:, e0 : e0 + width].bitcast(FP8X4), rhs_scale=h_s[c, g][:, e0 : e0 + width],
-                start=start, stop=stop,
-            )
-
-        out_rows = out.rearrange("(n p) e -> p n e", p=P)
-
-        def emit(bank, n0, count, e0, width, on_vector):
-            res = keep.tile([P, count, width], F32, name="res%d_%d" % (n0, e0))
-            sums = bank[:, 0 : count * width].rearrange("p (n e) -> p n e", n=count)
-            if on_vector:
-                shift = bm_sb[:, n0 : n0 + count].unsqueeze(2).broadcast_to([P, count, width])
-                nc.vector.tensor_tensor(res[:], sums, shift, ALU.add)
-            else:
-                for i in range(count):
-                    nc.scalar.activation(res[:, i, :], sums[:, i, :], ACT.Identity, bias=bm_sb[:, n0 + i : n0 + i + 1])
-            nc.sync.dma_start(out=out_rows[:, n0 : n0 + count, e0 : e0 + width], in_=res[:])
-
-        tail_banks = []
-        spare = [banks[1, t] for t in range(PACK)] + [banks[0, 0]]
-        for e0, width in TAIL:
-            count = NJ // width if e0 + width < NJ else 2
-            for n0 in range(0, N // P, count):
-                tail_banks.append((spare[len(tail_banks)], n0, count, e0, width))
-
-        def tail_passes(c, bank, n0, count, e0, width):
-            steps = [(i, d) for i in range(count) for d in range(0, width, P)]
-            for i, d in steps:
-                dst = bank[:, i * width + d : i * width + d + P]
-                pass_wm(dst, c, 1, n0 + i, e0 + d, P, c == 0 and (i, d) == steps[0], c == 1 and (i, d) == steps[-1])
-
-        on_scalar, on_vector = nc.scalar.copy, nc.vector.tensor_copy
-        gather(v2_w, tab2_w[:].bitcast(U32), idx2)
-        gather(v2_s, tab2_s[:].bitcast(U8), idx2)
-        nc.vector.tensor_copy(
-            wr_s[:].rearrange("p (t m) -> p t m", t=PACK),
-            wr_s_in[:].bitcast(U8).rearrange("p (m t) -> p t m", t=PACK),
-        )
-        v_w[0] = mid.tile([P, S], U32, name="v_w0", offset=4 * T, align_bytes=64)
-        gather(v_w[0], tab_w[0][:].bitcast(U32), idx)
         for g in range(2):
-            for t in range(PACK):
-                pass_wr(0, g, t)
-        prepare_ws(0, 0, (on_scalar, on_scalar))
-        for g in range(2):
-            for t in range(PACK):
-                pass_ws(0, 0, g, t)
-        gather(v_w[1], tab_w[1][:].bitcast(U32), idx)
-        prepare_ws(1, 0, (on_vector, on_scalar))
-        for t in range(PACK):
-            pass_ws(1, 0, 0, t)
-            tanh(0, 0, t)
-        for t in range(PACK):
-            pass_ws(1, 0, 1, t)
-            tanh(0, 1, t)
-        prepare_ws(0, 1, (on_vector, on_vector))
-        scale(0, 0, 0, P)
-        for half in range(2):
-            for u in range(2):
-                dst = ws_bf[1, 1, u][:].rearrange("p (t m j) -> p m j t", t=2, j=PACK)[:, half * P // 2 : (half + 1) * P // 2]
-                src = ws_last[half][:].rearrange("p j (m t) -> p m j t", t=PACK)
-                on_vector(dst, src[:, :, :, 2 * u : 2 * u + 2])
+            gather_words(1, g * NJ, NJ)
+        for bank, g, t in ahead:
+            pass_ws(bank, 1, 0, g, t, stop=True)
+            tanh(bank, 0, g, t)
+
+        prepare_ws(nc.vector.tensor_copy, 0, 1)
+        on_vector, on_scalar = nc.vector.tensor_copy, nc.scalar.copy
+        for half, u, copy in ((0, 0, on_vector), (0, 1, on_vector), (1, 0, on_vector), (1, 1, on_vector)):
+            regroup(copy, ws_last[half], 1, 1, u, half * P // 2, P // 2)
         for u in range(2):
             quantise_ws(1, 1, u)
-
-        def second_block(g):
-            for t in range(PACK):
-                pass_wr(1, g, t)
-                pass_ws(0, 1, g, t)
-                pass_ws(1, 1, g, t)
-                tanh(1, g, t)
-
-        second_block(0)
         for t in range(PACK):
-            pass_ws(1, 1, 1, t, True)
-            pass_wr(1, 1, t, False)
-            pass_ws(0, 1, 1, t, True)
-            tanh(1, 1, t)
-        scale_on_scalar(1, 1, *TAIL[0])
-        halves = ((0, NJ // 2), (NJ // 2, NJ // 2))
+            whole_sum(t, 1, 0, t)
+        for t, bank in enumerate((4, 5, 6, 7)):
+            pass_ws(bank, 1, 1, 1, t, start=True)
+            pass_wr(bank, 1, 1, t, start=False)
+            pass_ws(bank, 0, 1, 1, t, stop=True)
+            tanh(bank, 1, 1, t)
+
+        scale_on_scalar(1, NJ, P)
         for c in range(2):
+            for e0 in (0, NQ):
+                scale(c, e0, NQ)
+            for e0 in (0, NQ):
+                quantise_h(c, e0, NQ)
             if c == 0:
-                scale(0, 0, P, P)
-            else:
-                scale(1, 0, *halves[0])
-            scale(c, 0, *halves[1])
-            for part in halves:
-                quantise_h(c, 0, *part)
-            if c == 0:
-                scale(0, 1, *TAIL[0])
-            for n in range(N // P):
-                pass_wm(banks[0, n][:], c, 0, n, 0, NJ, c == 0, c == 1)
-        for n in range(N // P):
-            emit(banks[0, n], n, 1, 0, NJ, False)
-        h_bf[0, 1] = keep.tile([P, PACK * NJ], BF16, name="h_bf01", tag="act10", align_bytes=64)
-        for e0, width in TAIL:
-            if e0 > 0:
-                for c in range(2):
-                    scale(c, 1, e0, width)
+                scale(0, NJ, P)
+        messages(0, NJ, (0, 1, 2, 3))
+        for e0, width, where in ((NJ, P, (4,)), (NJ + P, NQ, (5, 6)), (S - P, P, (7, 0))):
+            if e0 > NJ:
+                scale(0, e0, width, "act10")
+                scale(1, e0, width)
             for c in range(2):
-                quantise_h(c, 1, e0, width)
-            here = [item for item in tail_banks if item[3] == e0]
-            for c in range(2):
-                for item in here:
-                    tail_passes(c, *item)
-            for item in here:
-                bank, n0, count = item[:3]
-                emit(bank, n0, count, NJ + e0, width, item is tail_banks[-1])
+                quantise_h(c, e0, width)
+            messages(e0, width, where, e0 + width == S)

@@ -102,7 +102,10 @@ def tile_list_bipartite_edge_messages_kernel(
         wr_rows = wr_scales[0].rearrange("(q r) (c n) -> q c r n", r=4, c=2)
         for q in range(4):
             nc.sync.dma_start(out=wr_s_in[32 * q + 8 : 32 * q + 16, :], in_=wr_rows[q].bitcast(I32))
-        permute_wr(1)
+        nc.scalar.copy(
+            wr_w[:, KP:H].bitcast(U32).rearrange("p (t m) -> p m t", t=PACK),
+            wr_in[1][:].bitcast(U32).rearrange("p (m t) -> p m t", t=PACK),
+        )
         ws_raw = {(0, 0): placed(4, 3 * KIB, "ws_raw00", [P, PACK, KP], F32)}
         load_ws(ws_raw[0, 0], 0, 0, KP)
 
@@ -251,7 +254,10 @@ def tile_list_bipartite_edge_messages_kernel(
         ahead = [(bank, bank // PACK, bank % PACK) for bank in range(8)]
         for bank, g, t in ahead:
             pass_wr(bank, 0, g, t)
-        prepare_ws(nc.scalar.copy, 0, 0)
+        regroup(nc.scalar.copy, ws_raw[0, 0], 0, 0, 0)
+        regroup(nc.vector.tensor_copy, ws_raw[0, 0], 0, 0, 1)
+        for u in range(2):
+            quantise_ws(0, 0, u)
         for t in range(PACK):
             pass_ws(t, 0, 0, 0, t)
         prepare_ws(nc.scalar.copy, 1, 0)

@@ -24,6 +24,7 @@ NQ = 256
 TAB2_ROW = 8
 WR_ROWS = (8, 12)
 RUN = 2
+PITCH = 384
 KIB = 1024
 
 
@@ -159,14 +160,14 @@ def tile_list_bipartite_edge_messages_kernel(
             for u in range(2):
                 quantise_ws(a, c, u)
 
-        def pass_wr(bank, c, g, t, start=True):
+        def pass_wr(bank, c, g, t, start=True, stop=False):
             cols = slice(c * KP + t * P, c * KP + (t + 1) * P)
             nc.tensor.matmul_mx(
                 out=banks[bank][:],
                 lhsT=wr_w[:, cols].bitcast(FP8X4), lhsT_scale=wr_s[WR_ROWS[c] : P, t * P : (t + 1) * P],
                 rhs=v2_w[g][:].bitcast(FP8X4),
                 rhs_scale=v2_s[TAB2_ROW:P, g * NJ : (g + 1) * NJ],
-                start=start, stop=False,
+                start=start, stop=stop,
             )
 
         def pass_ws(bank, a, c, g, t, start=False, stop=False):
@@ -265,11 +266,12 @@ def tile_list_bipartite_edge_messages_kernel(
         gather(v_w[0, NJ][:], tab_w[0][:].bitcast(U32), idx[:, NJ // 16 :])
         for bank, g, t in ahead[PACK:]:
             pass_ws(bank, 0, 0, g, t)
-        ws_last = [placed(0, 4 * KIB * half, "ws_last%d" % half, [P, PACK, KP // 2], F32) for half in range(2)]
-        wm_w = placed(0, 8 * KIB, "wm_w", [P, 2, N // 2], I32)
-        wm_s = placed(0, 10 * KIB, "wm_s", [P, 2, N // 4], I32)
-        bm_sb = placed(0, 11 * KIB, "bm_sb", [P, N // P], F32)
-        gain_sb = placed(0, 12 * KIB, "gain_sb", [P, 2, PACK], F32)
+        padded = [placed(0, 6 * KIB * half, "ws_last%d" % half, [P, PACK, PITCH], F32) for half in range(2)]
+        ws_last = [tile[:, :, 0 : KP // 2] for tile in padded]
+        wm_w = placed(0, 12 * KIB, "wm_w", [P, 2, N // 2], I32)
+        wm_s = placed(0, 14 * KIB, "wm_s", [P, 2, N // 4], I32)
+        bm_sb = placed(0, 15 * KIB, "bm_sb", [P, N // P], F32)
+        gain_sb = placed(0, 15 * KIB + 64, "gain_sb", [P, 2, PACK], F32)
         nc.vector.memset(wm_s[:], 0)
         for half in range(2):
             load_ws(ws_last[half], 1, KP + half * KP // 2, KP // 2)
@@ -295,7 +297,11 @@ def tile_list_bipartite_edge_messages_kernel(
             quantise_ws(1, 1, u)
         for t in range(PACK):
             whole_sum(t, 1, 0, t)
-        for t, bank in enumerate((4, 5, 6, 7)):
+        pass_ws(4, 0, 1, 1, 0, start=True)
+        pass_ws(4, 1, 1, 1, 0)
+        pass_wr(4, 1, 1, 0, start=False, stop=True)
+        tanh(4, 1, 1, 0)
+        for t, bank in ((1, 5), (2, 6), (3, 7)):
             pass_ws(bank, 1, 1, 1, t, start=True)
             pass_wr(bank, 1, 1, t, start=False)
             pass_ws(bank, 0, 1, 1, t, stop=True)

@@ -21,7 +21,6 @@ PACK = 4
 KP = P * PACK
 NJ = 512
 NQ = 256
-TAB2_ROW = 8
 WR_ROWS = (8, 12)
 RUN = 2
 PITCH = 384
@@ -35,7 +34,7 @@ def tile_list_bipartite_edge_messages_kernel(
     nc = tc.nc
     with ExitStack() as ctx:
         keep = ctx.enter_context(tc.tile_pool(name="keep", bufs=1))
-        rooms = [ctx.enter_context(tc.tile_pool(name="room%d" % i, bufs=1)) for i in range(5)]
+        rooms = [ctx.enter_context(tc.tile_pool(name="room%d" % i, bufs=1)) for i in range(6)]
         psum = ctx.enter_context(tc.psum_pool(name="psum", bufs=1))
 
         def held(name, shape, dtype, tag=None):
@@ -56,24 +55,23 @@ def tile_list_bipartite_edge_messages_kernel(
         tab2_s = placed(3, 0, "tab2_s", [P, T2 // 4], I32)
         wr_w = held("wr_w", [P, H], I32)
         wr_s = held("wr_s", [P, KP], U8)
-        v_s = [held("v_s%d" % a, [P, S // 4], I32) for a in range(2)]
+        v_s = [held("v_s%d" % a, [P, (2 - a) * S // 4], I32) for a in range(2)]
         pieces = [(a, c, u) for a in range(2) for c in range(2) for u in range(2)]
         ws_bf = {k: held("ws_bf%d%d%d" % k, [P, 2 * KP], BF16) for k in pieces}
         ws_w = {k: held("ws_w%d%d%d" % k, [P, 2 * P], U32) for k in pieces}
         ws_s = {k: held("ws_s%d%d%d" % k, [P, 2 * P], U8) for k in pieces}
 
-        for tile in (tab_s, tab2_s, v_s[0], v_s[1]):
+        nc.gpsimd.memset(tab2_s[:], 0)
+        for tile in (tab_s, v_s[0], v_s[1]):
             nc.vector.memset(tile[:], 0)
 
         for c in range(2):
             nc.sync.dma_start(out=wr_in[c][:], in_=words(wr_words[0])[:, c * KP : (c + 1) * KP])
         nc.sync.dma_start(idx2[:], offs2)
         nc.sync.dma_start(idx[:], offs)
+        nc.sync.dma_start(out=tab2_s[0 : P // 2 : 4, :], in_=tab2_scales[0].bitcast(I32))
         nc.sync.dma_start(out=tab_s[0:P:4, :], in_=tab_scales.rearrange("a q n -> (a q) n").bitcast(I32))
         nc.sync.dma_start(out=tab2_w[:], in_=words(tab2_words[0]))
-        tab2_rows = tab2_scales[0].rearrange("(q r) n -> r q n", r=4)
-        for r in range(4):
-            nc.sync.dma_start(out=tab2_s[TAB2_ROW + r : P : 32, :], in_=tab2_rows[r].bitcast(I32))
 
 
         def permute_wr(c):
@@ -92,17 +90,17 @@ def tile_list_bipartite_edge_messages_kernel(
 
         def carry(a):
             for r in range(4):
-                src = spread[64 * a + 4 * r : 64 * a + 64 : 16, :]
+                src = spread[64 * a + 4 * r : 64 * a + 64 : 16, 0 : (2 - a) * S]
                 nc.sync.dma_start(out=v_s[a][4 * a + r : P : 32, :], in_=src.bitcast(I32))
 
         permute_wr(0)
         tab_w = [placed(0, 0, "tab_w0", [P, T], I32)]
-        wr_s_in = placed(0, 16 * KIB, "wr_s_in", [P, KP // 4], I32)
-        nc.vector.memset(wr_s_in[:], 0)
+        wr_s_in = placed(5, 0, "wr_s_in", [P, 4, KP // 4], I32)
+        nc.vector.memset(wr_s_in[0:32], 0)
         nc.sync.dma_start(out=tab_w[0][:], in_=words(tab_words[0]))
-        wr_rows = wr_scales[0].rearrange("(q r) (c n) -> q c r n", r=4, c=2)
-        for q in range(4):
-            nc.sync.dma_start(out=wr_s_in[32 * q + 8 : 32 * q + 16, :], in_=wr_rows[q].bitcast(I32))
+        wr_rows = wr_scales[0].rearrange("(q r) (c n) -> c r q n", r=4, c=2)
+        for c in range(2):
+            nc.sync.dma_start(out=wr_s_in[WR_ROWS[c] : WR_ROWS[c] + 4], in_=wr_rows[c].bitcast(I32))
         nc.scalar.copy(
             wr_w[:, KP:H].bitcast(U32).rearrange("p (t m) -> p m t", t=PACK),
             wr_in[1][:].bitcast(U32).rearrange("p (m t) -> p m t", t=PACK),
@@ -110,28 +108,30 @@ def tile_list_bipartite_edge_messages_kernel(
         ws_raw = {(0, 0): placed(4, 3 * KIB, "ws_raw00", [P, PACK, KP], F32)}
         load_ws(ws_raw[0, 0], 0, 0, KP)
 
-        spread = placed(4, 2 * KIB, "spread", [P, S], U8)
-        gather(spread[:], tab_s[:].bitcast(U8), idx[:])
+        spread = placed(4, KIB, "spread", [P, 2 * S], U8)
+        gather(spread[:, S : 2 * S], tab2_s[:].bitcast(U8), idx2[:])
+        gather(spread[:, 0:S], tab_s[:].bitcast(U8), idx[:])
         ws_raw[1, 0] = placed(1, 0, "ws_raw10", [P, PACK, KP], F32)
-        b_sb = placed(1, 8 * KIB, "b_sb", [P, 2, PACK], F32)
+        b_sb = [placed(1, 8 * KIB, "b_sb0", [P, PACK], F32)]
+        b_rows = b.rearrange("(c p t) -> c p t", p=P, t=PACK)
         tab_w.append(placed(1, 11 * KIB + 64, "tab_w1", [P, T], I32))
-        load_ws(ws_raw[1, 0], 1, 0, KP)
         carry(0)
+        load_ws(ws_raw[1, 0], 1, 0, KP)
         nc.sync.dma_start(out=tab_w[1][:], in_=words(tab_words[1]))
         carry(1)
-        nc.sync.dma_start(out=b_sb[:], in_=b.rearrange("(c p t) -> p c t", p=P, t=PACK))
+        nc.sync.dma_start(out=b_sb[0][:], in_=b_rows[0])
 
         v2_w = [placed(1, 8 * KIB + 64, "v2_w0", [P, NJ], U32)]
-        v2_s = placed(1, 10 * KIB + 64, "v2_s", [P, S], U8)
         gather(v2_w[0][:], tab2_w[:].bitcast(U32), idx2[:, 0 : NJ // 16])
-        gather(v2_s[:], tab2_s[:].bitcast(U8), idx2[:])
         v2_w.append(placed(3, 0, "v2_w1", [P, NJ], U32))
         gather(v2_w[1][:], tab2_w[:].bitcast(U32), idx2[:, NJ // 16 :])
         ws_raw[0, 1] = placed(2, 0, "ws_raw01", [P, PACK, KP], F32)
         load_ws(ws_raw[0, 1], 0, KP, KP)
+        for q in range(1, 4):
+            nc.vector.tensor_copy(wr_s_in[32 * q : 32 * (q + 1), 0, :], wr_s_in[0:32, q, :])
         nc.vector.tensor_copy(
             wr_s[:].rearrange("p (t m) -> p t m", t=PACK),
-            wr_s_in[:].bitcast(U8).rearrange("p (m t) -> p t m", t=PACK),
+            wr_s_in[:, 0, :].bitcast(U8).rearrange("p (m t) -> p t m", t=PACK),
         )
 
         v_w = {}
@@ -144,7 +144,7 @@ def tile_list_bipartite_edge_messages_kernel(
             first = max(k[1] for k in v_w if k[0] == a and k[1] <= e0)
             return v_w[a, first][:, e0 - first : e0 - first + width]
 
-        v_w[0, 0] = placed(0, 16 * KIB, "v_w0", [P, NJ], U32)
+        v_w[0, 0] = placed(5, 0, "v_w0", [P, NJ], U32)
         gather(v_w[0, 0][:], tab_w[0][:].bitcast(U32), idx[:, 0 : NJ // 16])
         def regroup(copy, raw, a, c, u, m0=0, count=P):
             dst = ws_bf[a, c, u][:].rearrange("p (t m j) -> p m j t", t=2, j=PACK)[:, m0 : m0 + count]
@@ -166,7 +166,7 @@ def tile_list_bipartite_edge_messages_kernel(
                 out=banks[bank][:],
                 lhsT=wr_w[:, cols].bitcast(FP8X4), lhsT_scale=wr_s[WR_ROWS[c] : P, t * P : (t + 1) * P],
                 rhs=v2_w[g][:].bitcast(FP8X4),
-                rhs_scale=v2_s[TAB2_ROW:P, g * NJ : (g + 1) * NJ],
+                rhs_scale=v_s[0][:].bitcast(U8)[:, S + g * NJ : S + (g + 1) * NJ],
                 start=start, stop=stop,
             )
 
@@ -185,7 +185,7 @@ def tile_list_bipartite_edge_messages_kernel(
         h_s = {k: held("h_s%d%d" % k, [P, NJ], U8) for k in act}
 
         def tanh(bank, c, g, t):
-            nc.scalar.activation(act[c, g][:, t, :], banks[bank][:], ACT.Tanh, bias=b_sb[:, c, t : t + 1])
+            nc.scalar.activation(act[c, g][:, t, :], banks[bank][:], ACT.Tanh, bias=b_sb[c][:, t : t + 1])
 
         def whole_sum(bank, c, g, t):
             pass_wr(bank, c, g, t)
@@ -275,6 +275,8 @@ def tile_list_bipartite_edge_messages_kernel(
         nc.vector.memset(wm_s[:], 0)
         for half in range(2):
             load_ws(ws_last[half], 1, KP + half * KP // 2, KP // 2)
+        b_sb.append(placed(0, 15 * KIB + 128, "b_sb1", [P, PACK], F32))
+        nc.sync.dma_start(out=b_sb[1][:], in_=b_rows[1])
         nc.sync.dma_start(out=gain_sb[:], in_=gain.rearrange("(c p t) -> p c t", p=P, t=PACK))
         nc.sync.dma_start(out=wm_w[:], in_=wm_words.rearrange("a p n -> p a n").bitcast(I32))
         with nc.allow_non_contiguous_dma(reason="one bias value a partition"):

@@ -49,9 +49,9 @@ def tile_list_bipartite_edge_messages_kernel(
         idx = keep.tile([P, S // 16], U16, name="idx")
         idx2 = keep.tile([P, S // 16], U16, name="idx2")
         banks = [psum.tile([P, NJ], F32, name="bank%d" % i) for i in range(8)]
-        wr_in = [placed(0, 15 * KIB, "wr_in0", [P, KP], I32), placed(4, 2 * KIB - 64, "wr_in1", [P, KP], I32)]
+        wr_in = [placed(0, 16 * KIB - 64, "wr_in0", [P, KP], I32)]
         tab_s = placed(1, 8 * KIB - 64, "tab_s", [P, T // 4], I32)
-        tab2_w = placed(2, 0, "tab2_w", [P, T2], I32)
+        tab2_w = placed(2, 2 * KIB, "tab2_w", [P, T2], I32)
         tab2_s = placed(3, 0, "tab2_s", [P, T2 // 4], I32)
         wr_w = held("wr_w", [P, H], I32)
         wr_s = held("wr_s", [P, KP], U8)
@@ -65,13 +65,13 @@ def tile_list_bipartite_edge_messages_kernel(
         for tile in (tab_s, v_s[0], v_s[1]):
             nc.vector.memset(tile[:], 0)
 
-        for c in range(2):
-            nc.sync.dma_start(out=wr_in[c][:], in_=words(wr_words[0])[:, c * KP : (c + 1) * KP])
+        nc.sync.dma_start(out=wr_in[0][:], in_=words(wr_words[0])[:, 0:KP])
+        nc.sync.dma_start(out=tab2_w[:, 0 : T2 // 2], in_=words(tab2_words[0])[:, 0 : T2 // 2])
         nc.sync.dma_start(idx2[:], offs2)
         nc.sync.dma_start(idx[:], offs)
         nc.sync.dma_start(out=tab2_s[0 : P // 2 : 4, :], in_=tab2_scales[0].bitcast(I32))
         nc.sync.dma_start(out=tab_s[0:P:4, :], in_=tab_scales.rearrange("a q n -> (a q) n").bitcast(I32))
-        nc.sync.dma_start(out=tab2_w[:], in_=words(tab2_words[0]))
+        nc.sync.dma_start(out=tab2_w[:, T2 // 2 :], in_=words(tab2_words[0])[:, T2 // 2 :])
 
 
         def permute_wr(c):
@@ -101,11 +101,7 @@ def tile_list_bipartite_edge_messages_kernel(
         wr_rows = wr_scales[0].rearrange("(q r) (c n) -> c r q n", r=4, c=2)
         for c in range(2):
             nc.sync.dma_start(out=wr_s_in[WR_ROWS[c] : WR_ROWS[c] + 4], in_=wr_rows[c].bitcast(I32))
-        nc.scalar.copy(
-            wr_w[:, KP:H].bitcast(U32).rearrange("p (t m) -> p m t", t=PACK),
-            wr_in[1][:].bitcast(U32).rearrange("p (m t) -> p m t", t=PACK),
-        )
-        ws_raw = {(0, 0): placed(4, 3 * KIB, "ws_raw00", [P, PACK, KP], F32)}
+        ws_raw = {(0, 0): placed(0, 16 * KIB, "ws_raw00", [P, PACK, KP], F32)}
         load_ws(ws_raw[0, 0], 0, 0, KP)
 
         spread = placed(4, KIB, "spread", [P, 2 * S], U8)
@@ -125,8 +121,10 @@ def tile_list_bipartite_edge_messages_kernel(
         gather(v2_w[0][:], tab2_w[:].bitcast(U32), idx2[:, 0 : NJ // 16])
         v2_w.append(placed(3, 0, "v2_w1", [P, NJ], U32))
         gather(v2_w[1][:], tab2_w[:].bitcast(U32), idx2[:, NJ // 16 :])
-        ws_raw[0, 1] = placed(2, 0, "ws_raw01", [P, PACK, KP], F32)
+        ws_raw[0, 1] = placed(2, 2 * KIB + 64, "ws_raw01", [P, PACK, KP], F32)
         load_ws(ws_raw[0, 1], 0, KP, KP)
+        wr_in.append(placed(2, 64, "wr_in1", [P, KP], I32))
+        nc.sync.dma_start(out=wr_in[1][:], in_=words(wr_words[0])[:, KP:H])
         for q in range(1, 4):
             nc.vector.tensor_copy(wr_s_in[32 * q : 32 * (q + 1), 0, :], wr_s_in[0:32, q, :])
         nc.vector.tensor_copy(
@@ -188,8 +186,8 @@ def tile_list_bipartite_edge_messages_kernel(
             nc.scalar.activation(act[c, g][:, t, :], banks[bank][:], ACT.Tanh, bias=b_sb[c][:, t : t + 1])
 
         def whole_sum(bank, c, g, t):
-            pass_wr(bank, c, g, t)
-            pass_ws(bank, 0, c, g, t)
+            pass_ws(bank, 0, c, g, t, start=True)
+            pass_wr(bank, c, g, t, start=False)
             pass_ws(bank, 1, c, g, t, stop=True)
             tanh(bank, c, g, t)
 
@@ -219,13 +217,12 @@ def tile_list_bipartite_edge_messages_kernel(
             cols = slice(first, first + width)
             nc.vector.quantize_mx(out=h_w[c, g][:, cols].bitcast(FP8X4), scales=h_s[c, g][:, cols], in_=h_bf[c, e0][:])
 
-        def second_product(c, e0, width, where):
+        def second_product(c, e0, width, bank, n0, count):
             g, first = divmod(e0, NJ)
-            count = N // P // len(where)
-            for n in range(N // P):
-                i = n % count
+            for i in range(count):
+                n = n0 + i
                 nc.tensor.matmul_mx(
-                    out=banks[where[n // count]][:, i * width : (i + 1) * width],
+                    out=banks[bank][:, i * width : (i + 1) * width],
                     lhsT=wm_w[:, c, :].bitcast(U8)[:, 2 * n * P : 2 * (n + 1) * P].bitcast(FP4X4),
                     lhsT_scale=wm_s[:, c, :].bitcast(U8)[:, n * P : (n + 1) * P],
                     rhs=h_w[c, g][:, first : first + width].bitcast(FP8X4), rhs_scale=h_s[c, g][:, first : first + width],
@@ -246,10 +243,10 @@ def tile_list_bipartite_edge_messages_kernel(
             nc.sync.dma_start(out=out_rows[:, n0 : n0 + count, e0 : e0 + width], in_=res[:])
 
         def messages(e0, width, where, last=False):
-            for c in range(2):
-                second_product(c, e0, width, where)
             count = N // P // len(where)
             for k, bank in enumerate(where):
+                for c in range(2):
+                    second_product(c, e0, width, bank, k * count, count)
                 emit(bank, k * count, count, e0, width, last and k == 1)
 
         ahead = [(bank, bank // PACK, bank % PACK) for bank in range(8)]
@@ -292,6 +289,7 @@ def tile_list_bipartite_edge_messages_kernel(
             tanh(bank, 0, g, t)
 
         prepare_ws(nc.vector.tensor_copy, 0, 1)
+        permute_wr(1)
         on_vector, on_scalar = nc.vector.tensor_copy, nc.scalar.copy
         for half, u, copy in ((0, 0, on_vector), (0, 1, on_vector), (1, 0, on_vector), (1, 1, on_vector)):
             regroup(copy, ws_last[half], 1, 1, u, half * P // 2, P // 2)

from contextlib import ExitStack

import concourse.mybir as mybir

K, K2, T, T2, S, H, N = 1024, 512, 4096, 2048, 1024, 1024, 512
FLOPS = 2 * S * (K * H + K2 * H + H * N)

F32 = mybir.dt.float32
BF16 = mybir.dt.bfloat16
I32 = mybir.dt.int32
U32 = mybir.dt.uint32
U16 = mybir.dt.uint16
U8 = mybir.dt.uint8
FP8X4 = mybir.dt.float8_e4m3fn_x4
FP4X4 = mybir.dt.float4_e2m1fn_x4
ACT = mybir.ActivationFunctionType
ALU = mybir.AluOpType

P = 128
PACK = 4
KP = P * PACK
NJ = 512
NQ = 256
WR_ROWS = (8, 12)
RUN = 2
PITCH = 384
KIB = 1024


def tile_list_bipartite_edge_messages_kernel(
    tc, tab_words, tab_scales, tab2_words, tab2_scales, offs, offs2, ws, wr_words, wr_scales,
    b, gain, wm_words, wm_scales, bm, out,
):
    nc = tc.nc
    with ExitStack() as ctx:
        keep = ctx.enter_context(tc.tile_pool(name="keep", bufs=1))
        rooms = [ctx.enter_context(tc.tile_pool(name="room%d" % i, bufs=1)) for i in range(6)]
        psum = ctx.enter_context(tc.psum_pool(name="psum", bufs=1))

        def held(name, shape, dtype, tag=None):
            return keep.tile(shape, dtype, name=name, tag=tag or name, align_bytes=64)

        def placed(room, offset, name, shape, dtype):
            return rooms[room].tile(shape, dtype, name=name, offset=offset, align_bytes=64)

        def words(ap):
            return ap.rearrange("p n i -> p (n i)").bitcast(I32)

        idx = keep.tile([P, S // 16], U16, name="idx")
        idx2 = keep.tile([P, S // 16], U16, name="idx2")
        banks = [psum.tile([P, NJ], F32, name="bank%d" % i) for i in range(8)]
        wr_in = [placed(0, 16 * KIB - 64, "wr_in0", [P, KP], I32)]
        tab_s = placed(1, 8 * KIB - 64, "tab_s", [P, T // 4], I32)
        tab2_w = placed(2, 2 * KIB, "tab2_w", [P, T2], I32)
        tab2_s = placed(3, 0, "tab2_s", [P, T2 // 4], I32)
        wr_w = held("wr_w", [P, H], I32)
        wr_s = held("wr_s", [P, KP], U8)
        v_s = [held("v_s%d" % a, [P, (2 - a) * S // 4], I32) for a in range(2)]
        pieces = [(a, c, u) for a in range(2) for c in range(2) for u in range(2)]
        ws_bf = {k: held("ws_bf%d%d%d" % k, [P, 2 * KP], BF16) for k in pieces}
        ws_w = {k: held("ws_w%d%d%d" % k, [P, 2 * P], U32) for k in pieces}
        ws_s = {k: held("ws_s%d%d%d" % k, [P, 2 * P], U8) for k in pieces}

        nc.gpsimd.memset(tab2_s[:], 0)
        for tile in (tab_s, v_s[0], v_s[1]):
            nc.vector.memset(tile[:], 0)

        nc.sync.dma_start(out=wr_in[0][:], in_=words(wr_words[0])[:, 0:KP])
        nc.sync.dma_start(out=tab2_w[:, 0 : T2 // 2], in_=words(tab2_words[0])[:, 0 : T2 // 2])
        nc.sync.dma_start(idx2[:], offs2)
        nc.sync.dma_start(idx[:], offs)
        nc.sync.dma_start(out=tab2_s[0 : P // 2 : 4, :], in_=tab2_scales[0].bitcast(I32))
        nc.sync.dma_start(out=tab_s[0:P:4, :], in_=tab_scales.rearrange("a q n -> (a q) n").bitcast(I32))
        nc.sync.dma_start(out=tab2_w[:, T2 // 2 :], in_=words(tab2_words[0])[:, T2 // 2 :])


        def permute_wr(c):
            dst = wr_w[:, c * KP : (c + 1) * KP].rearrange("p (t m) -> p m t", t=PACK)
            src = wr_in[c][:].rearrange("p (m t) -> p m t", t=PACK)
            for t0 in (0, 2):
                nc.vector.tensor_copy(dst[:, :, t0 : t0 + 2], src[:, :, t0 : t0 + 2])

        ws_rows = ws.rearrange("(a p j) r -> a p j r", a=2, j=PACK)

        def load_ws(tile, a, c0, width):
            nc.sync.dma_start(out=tile[:], in_=ws_rows[a][:, :, c0 : c0 + width])

        def gather(dst, window, offsets):
            nc.vector.tensor_copy(dst, window.indirect(offsets))

        def carry(a):
            for r in range(4):
                src = spread[64 * a + 4 * r : 64 * a + 64 : 16, 0 : (2 - a) * S]
                nc.sync.dma_start(out=v_s[a][4 * a + r : P : 32, :], in_=src.bitcast(I32))

        permute_wr(0)
        tab_w = [placed(0, 0, "tab_w0", [P, T], I32)]
        wr_s_in = placed(5, 0, "wr_s_in", [P, 4, KP // 4], I32)
        nc.vector.memset(wr_s_in[0:32], 0)
        nc.sync.dma_start(out=tab_w[0][:], in_=words(tab_words[0]))
        wr_rows = wr_scales[0].rearrange("(q r) (c n) -> c r q n", r=4, c=2)
        for c in range(2):
            nc.sync.dma_start(out=wr_s_in[WR_ROWS[c] : WR_ROWS[c] + 4], in_=wr_rows[c].bitcast(I32))
        ws_raw = {(0, 0): placed(0, 16 * KIB, "ws_raw00", [P, PACK, KP], F32)}
        load_ws(ws_raw[0, 0], 0, 0, KP)

        spread = placed(4, KIB, "spread", [P, 2 * S], U8)
        gather(spread[:, S : 2 * S], tab2_s[:].bitcast(U8), idx2[:])
        gather(spread[:, 0:S], tab_s[:].bitcast(U8), idx[:])
        ws_raw[1, 0] = placed(1, 0, "ws_raw10", [P, PACK, KP], F32)
        b_sb = [placed(1, 8 * KIB, "b_sb0", [P, PACK], F32)]
        b_rows = b.rearrange("(c p t) -> c p t", p=P, t=PACK)
        tab_w.append(placed(1, 11 * KIB + 64, "tab_w1", [P, T], I32))
        carry(0)
        load_ws(ws_raw[1, 0], 1, 0, KP)
        nc.sync.dma_start(out=tab_w[1][:], in_=words(tab_words[1]))
        carry(1)
        nc.sync.dma_start(out=b_sb[0][:], in_=b_rows[0])

        v2_w = [placed(1, 8 * KIB + 64, "v2_w0", [P, NJ], U32)]
        gather(v2_w[0][:], tab2_w[:].bitcast(U32), idx2[:, 0 : NJ // 16])
        v2_w.append(placed(3, 0, "v2_w1", [P, NJ], U32))
        gather(v2_w[1][:], tab2_w[:].bitcast(U32), idx2[:, NJ // 16 :])
        ws_raw[0, 1] = placed(2, 2 * KIB + 64, "ws_raw01", [P, PACK, KP], F32)
        load_ws(ws_raw[0, 1], 0, KP, KP)
        wr_in.append(placed(2, 64, "wr_in1", [P, KP], I32))
        nc.sync.dma_start(out=wr_in[1][:], in_=words(wr_words[0])[:, KP:H])
        for q in range(1, 4):
            nc.vector.tensor_copy(wr_s_in[32 * q : 32 * (q + 1), 0, :], wr_s_in[0:32, q, :])
        nc.vector.tensor_copy(
            wr_s[:].rearrange("p (t m) -> p t m", t=PACK),
            wr_s_in[:, 0, :].bitcast(U8).rearrange("p (m t) -> p t m", t=PACK),
        )

        v_w = {}

        def gather_words(a, e0, width):
            v_w[a, e0] = held("v_w%d_%d" % (a, e0), [P, width], U32)
            gather(v_w[a, e0][:], tab_w[a][:].bitcast(U32), idx[:, e0 // 16 : (e0 + width) // 16])

        def looked_up(a, e0, width):
            first = max(k[1] for k in v_w if k[0] == a and k[1] <= e0)
            return v_w[a, first][:, e0 - first : e0 - first + width]

        v_w[0, 0] = placed(5, 0, "v_w0", [P, NJ], U32)
        gather(v_w[0, 0][:], tab_w[0][:].bitcast(U32), idx[:, 0 : NJ // 16])
        def regroup(copy, raw, a, c, u, m0=0, count=P):
            dst = ws_bf[a, c, u][:].rearrange("p (t m j) -> p m j t", t=2, j=PACK)[:, m0 : m0 + count]
            src = raw[:].rearrange("p j (m t) -> p m j t", t=PACK)
            copy(dst, src[:, :, :, 2 * u : 2 * u + 2])

        def quantise_ws(a, c, u):
            nc.vector.quantize_mx(out=ws_w[a, c, u][:].bitcast(FP8X4), scales=ws_s[a, c, u][:], in_=ws_bf[a, c, u][:])

        def prepare_ws(copy, a, c):
            for u in range(2):
                regroup(copy, ws_raw[a, c], a, c, u)
            for u in range(2):
                quantise_ws(a, c, u)

        def pass_wr(bank, c, g, t, start=True, stop=False):
            cols = slice(c * KP + t * P, c * KP + (t + 1) * P)
            nc.tensor.matmul_mx(
                out=banks[bank][:],
                lhsT=wr_w[:, cols].bitcast(FP8X4), lhsT_scale=wr_s[WR_ROWS[c] : P, t * P : (t + 1) * P],
                rhs=v2_w[g][:].bitcast(FP8X4),
                rhs_scale=v_s[0][:].bitcast(U8)[:, S + g * NJ : S + (g + 1) * NJ],
                start=start, stop=stop,
            )

        def pass_ws(bank, a, c, g, t, start=False, stop=False):
            cols = slice(t % 2 * P, (t % 2 + 1) * P)
            nc.tensor.matmul_mx(
                out=banks[bank][:],
                lhsT=ws_w[a, c, t // 2][:, cols].bitcast(FP8X4), lhsT_scale=ws_s[a, c, t // 2][:, cols],
                rhs=looked_up(a, g * NJ, NJ).bitcast(FP8X4),
                rhs_scale=v_s[a][:].bitcast(U8)[4 * a : P, g * NJ : (g + 1) * NJ],
                start=start, stop=stop,
            )

        act = {(c, g): held("act%d%d" % (c, g), [P, PACK, NJ], F32) for c in range(2) for g in range(2)}
        h_w = {k: held("h_w%d%d" % k, [P, NJ], U32) for k in act}
        h_s = {k: held("h_s%d%d" % k, [P, NJ], U8) for k in act}

        def tanh(bank, c, g, t):
            nc.scalar.activation(act[c, g][:, t, :], banks[bank][:], ACT.Tanh, bias=b_sb[c][:, t : t + 1])

        def whole_sum(bank, c, g, t):
            pass_ws(bank, 0, c, g, t, start=True)
            pass_wr(bank, c, g, t, start=False)
            pass_ws(bank, 1, c, g, t, stop=True)
            tanh(bank, c, g, t)

        h_bf = {}

        def scale(c, e0, width, tag=None):
            g, first = divmod(e0, NJ)
            h_bf[c, e0] = held("h_bf%d_%d" % (c, e0), [P, PACK * width], BF16, tag)
            dst = h_bf[c, e0][:].rearrange("p (u i t) -> p u t i", i=RUN, t=PACK)
            src = act[c, g][:, :, first : first + width].rearrange("p t (u i) -> p u t i", i=RUN)
            factor = gain_sb[:, c, :].unsqueeze(1).unsqueeze(3).broadcast_to([P, width // RUN, PACK, RUN])
            nc.vector.tensor_tensor(dst, src, factor, ALU.mult)

        def scale_on_scalar(c, e0, width):
            g, first = divmod(e0, NJ)
            planes = held("planes", [P, PACK, width], BF16)
            for t in range(PACK):
                nc.scalar.activation(
                    planes[:, t, :], act[c, g][:, t, first : first + width], ACT.Copy, scale=gain_sb[:, c, t : t + 1]
                )
            h_bf[c, e0] = held("h_bf%d_%d" % (c, e0), [P, PACK * width], BF16)
            dst = h_bf[c, e0][:].rearrange("p (u i t) -> p u t i", i=4, t=PACK)
            nc.scalar.copy(dst, planes[:].rearrange("p t (u i) -> p u t i", i=4))

        def quantise_h(c, e0, width):
            g, first = divmod(e0, NJ)
            cols = slice(first, first + width)
            nc.vector.quantize_mx(out=h_w[c, g][:, cols].bitcast(FP8X4), scales=h_s[c, g][:, cols], in_=h_bf[c, e0][:])

        def second_product(c, e0, width, bank, n0, count):
            g, first = divmod(e0, NJ)
            for i in range(count):
                n = n0 + i
                nc.tensor.matmul_mx(
                    out=banks[bank][:, i * width : (i + 1) * width],
                    lhsT=wm_w[:, c, :].bitcast(U8)[:, 2 * n * P : 2 * (n + 1) * P].bitcast(FP4X4),
                    lhsT_scale=wm_s[:, c, :].bitcast(U8)[:, n * P : (n + 1) * P],
                    rhs=h_w[c, g][:, first : first + width].bitcast(FP8X4), rhs_scale=h_s[c, g][:, first : first + width],
                    start=(c == 0 and i == 0), stop=(c == 1 and i == count - 1),
                )

        out_rows = out.rearrange("(n p) e -> p n e", p=P)

        def emit(bank, n0, count, e0, width, on_vector=False):
            res = keep.tile([P, count, width], F32, name="res%d_%d" % (n0, e0))
            done = banks[bank][:, 0 : count * width].rearrange("p (n e) -> p n e", n=count)
            if on_vector:
                shift = bm_sb[:, n0 : n0 + count].unsqueeze(2).broadcast_to([P, count, width])
                nc.vector.tensor_tensor(res[:], done, shift, ALU.add)
            else:
                for i in range(count):
                    nc.scalar.activation(res[:, i, :], done[:, i, :], ACT.Identity, bias=bm_sb[:, n0 + i : n0 + i + 1])
            nc.sync.dma_start(out=out_rows[:, n0 : n0 + count, e0 : e0 + width], in_=res[:])

        def messages(e0, width, where, last=False):
            count = N // P // len(where)
            for k, bank in enumerate(where):
                for c in range(2):
                    second_product(c, e0, width, bank, k * count, count)
                emit(bank, k * count, count, e0, width, last and k == 1)

        ahead = [(bank, bank // PACK, bank % PACK) for bank in range(8)]
        for bank, g, t in ahead:
            pass_wr(bank, 0, g, t)
        regroup(nc.scalar.copy, ws_raw[0, 0], 0, 0, 0)
        regroup(nc.vector.tensor_copy, ws_raw[0, 0], 0, 0, 1)
        for u in range(2):
            quantise_ws(0, 0, u)
        for t in range(PACK):
            pass_ws(t, 0, 0, 0, t)
        prepare_ws(nc.scalar.copy, 1, 0)
        v_w[0, NJ] = held("v_w0_last", [P, NJ], U32, "ws_bf100")
        gather(v_w[0, NJ][:], tab_w[0][:].bitcast(U32), idx[:, NJ // 16 :])
        for bank, g, t in ahead[PACK:]:
            pass_ws(bank, 0, 0, g, t)
        padded = [placed(0, 6 * KIB * half, "ws_last%d" % half, [P, PACK, PITCH], F32) for half in range(2)]
        ws_last = [tile[:, :, 0 : KP // 2] for tile in padded]
        wm_w = placed(0, 12 * KIB, "wm_w", [P, 2, N // 2], I32)
        wm_s = placed(0, 14 * KIB, "wm_s", [P, 2, N // 4], I32)
        bm_sb = placed(0, 15 * KIB, "bm_sb", [P, N // P], F32)
        gain_sb = placed(0, 15 * KIB + 64, "gain_sb", [P, 2, PACK], F32)
        nc.vector.memset(wm_s[:], 0)
        for half in range(2):
            load_ws(ws_last[half], 1, KP + half * KP // 2, KP // 2)
        b_sb.append(placed(0, 15 * KIB + 128, "b_sb1", [P, PACK], F32))
        nc.sync.dma_start(out=b_sb[1][:], in_=b_rows[1])
        nc.sync.dma_start(out=gain_sb[:], in_=gain.rearrange("(c p t) -> p c t", p=P, t=PACK))
        nc.sync.dma_start(out=wm_w[:], in_=wm_words.rearrange("a p n -> p a n").bitcast(I32))
        with nc.allow_non_contiguous_dma(reason="one bias value a partition"):
            nc.sync.dma_start(out=bm_sb[:], in_=bm.rearrange("(c p) -> p c", p=P))
        wm_rows = wm_scales.rearrange("a (q r) n -> r q a n", r=4)
        for r in range(4):
            nc.sync.dma_start(out=wm_s[r:P:32, :, :], in_=wm_rows[r].bitcast(I32))

        for g in range(2):
            gather_words(1, g * NJ, NJ)
        for bank, g, t in ahead:
            pass_ws(bank, 1, 0, g, t, stop=True)
            tanh(bank, 0, g, t)

        prepare_ws(nc.vector.tensor_copy, 0, 1)
        permute_wr(1)
        on_vector, on_scalar = nc.vector.tensor_copy, nc.scalar.copy
        for half, u, copy in ((0, 0, on_vector), (0, 1, on_vector), (1, 0, on_vector), (1, 1, on_vector)):
            regroup(copy, ws_last[half], 1, 1, u, half * P // 2, P // 2)
        for u in range(2):
            quantise_ws(1, 1, u)
        for t in range(PACK):
            whole_sum(t, 1, 0, t)
        pass_ws(4, 0, 1, 1, 0, start=True)
        pass_ws(4, 1, 1, 1, 0)
        pass_wr(4, 1, 1, 0, start=False, stop=True)
        tanh(4, 1, 1, 0)
        for t, bank in ((1, 5), (2, 6), (3, 7)):
            pass_ws(bank, 1, 1, 1, t, start=True)
            pass_wr(bank, 1, 1, t, start=False)
            pass_ws(bank, 0, 1, 1, t, stop=True)
            tanh(bank, 1, 1, t)

        scale_on_scalar(1, NJ, P)
        for c in range(2):
            for e0 in (0, NQ):
                scale(c, e0, NQ)
            for e0 in (0, NQ):
                quantise_h(c, e0, NQ)
            if c == 0:
                scale(0, NJ, P)
        messages(0, NJ, (0, 1, 2, 3))
        for e0, width, where in ((NJ, P, (4,)), (NJ + P, NQ, (5, 6)), (S - P, P, (7, 0))):
            if e0 > NJ:
                scale(0, e0, width, "act10")
                scale(1, e0, width)
            for c in range(2):
                quantise_h(c, e0, width)
            messages(e0, width, where, e0 + width == S)
